import numpy as np, ml_dtypes
CORES = [66,74,82,90,194,202,210,218]
N = 8
BF = ml_dtypes.bfloat16
W, A, L, S, Q, C = 2048, 4, 3, 5, 96, 32
def place(x, wv, kv):
    u = np.sum(wv * x, axis=2) & (W - 1)
    return (((u * u) >> 5)[..., None] + kv[:, :, None, :] * u[..., None]) & (W - 1)
def search(X, q, wv, kv):
    n, m = q.shape[0], q.shape[3]
    pl = place(q, wv, kv); ok = np.ones(pl.shape, bool); line = [pl]; levels, dist = [], []
    for l in range(L):
        k = A ** (l + 1)
        occ = np.take_along_axis(X, pl.reshape(n, 8, 1, m * k), 3)
        d = np.sum(np.abs(occ.reshape(n, 8, 16, m, k) - q[..., None]), axis=2)
        if l == 0: hit = np.any(d == 0, axis=3)
        levels.append(pl); dist.append(np.where(ok, d, -1))
        if l < L - 1:
            good = ok & (occ[:, :, 0].reshape(n, 8, m, k) != 512)
            pl = place(occ, wv, kv).reshape(n, 8, m, k * A)
            line = [np.repeat(a, A, axis=3) for a in line]
            ok = np.repeat(good, A, axis=3)
            for a in line: ok = ok & (pl != a)
            line.append(pl)
    D = np.concatenate(dist, axis=3); v = D.shape[3] - 1 - np.argmax(D[..., ::-1], axis=3)
    path = np.full((n, 8, m, L), -1, np.int64); depth = np.zeros((n, 8, m), np.int64); base = 0
    for l in range(L):
        k = A ** (l + 1); here = (v >= base) & (v < base + k); j = np.clip(v - base, 0, k - 1)
        for h in range(l + 1):
            t = np.take_along_axis(levels[h], (j // A ** (l - h))[..., None], 3)[..., 0]
            path[..., h] = np.where(here, t, path[..., h])
        depth = np.where(here, l, depth); base += k
    return (q[:, :, 0] != 512) & ~hit, depth, path
def step(X, q, wv, kv):
    n, m = q.shape[0], q.shape[3]
    live, depth, path = search(X, q, wv, kv)
    meet = np.zeros((n, 8, m, m), bool)
    for a in range(L):
        for b in range(L):
            meet |= (path[..., a][..., :, None] == path[..., b][..., None, :]) & (path[..., a] >= 0)[..., None]
    go = live & ~np.any(meet & live[:, :, None, :] & np.tri(m, m, -1, dtype=bool), axis=3)
    old = [np.take_along_axis(X, np.maximum(path[..., l], 0)[:, :, None, :], 3) for l in range(L)]
    Y = X.copy(); val = q; vic = old[0]
    for l in range(L):
        r, g, i = np.nonzero(go & (depth >= l))
        Y[r, g, :, path[r, g, i, l]] = val[r, g, :, i]; val = old[l]
        vic = np.where((depth >= l)[:, :, None, :], old[l], vic)
    gone = go & (vic[:, :, 0] != 512); slot = np.add.accumulate(gone.astype(np.int64), axis=2) - 1
    out = np.full((n, 8, 16, C), 512, np.int32); r, g, i = np.nonzero(gone & (slot < C))
    out[r, g, :, slot[r, g, i]] = vic[r, g, :, i]
    return Y, out
def records(rng, k): return rng.integers(0, 256, (N, 8, 16, k)).astype(np.int32)
def hashes(rng): return rng.integers(1, 256, (N, 8, 16, 1)).astype(np.int32), 2 * rng.integers(0, 1024, (N, 8, A)) + 1
def fill(rng, rec, wv, kv, full, bare):
    pl = place(rec, wv, kv); k = rec.shape[3]; X = np.full((N, 8, 16, W), 512, np.int32)
    for r in range(N):
        for g in range(8):
            own = np.full(W, -1); free = np.arange(k)
            for a in range(A):
                p = pl[r, g, free, a]; e = own[p] < 0; own[p[e]] = free[e]; free = free[own[p] != free]
            if full[r, g]: own = np.where(own < 0, rng.integers(0, k, W), own)
            own = np.where(rng.random(W) < bare[r, g], -1, own)
            X[r, g] = np.where(own >= 0, rec[r, g][:, own], 512)
    return X
def ask(rng, X, fresh):
    c = rng.integers(0, W, (N, 8, 1, S * Q)); v = np.take_along_axis(X, c, 3).reshape(N, 8, 16, S, Q)
    q = np.where((rng.random((N, 8, 1, S, Q)) < 0.2) & (v[:, :, :1] != 512), v, fresh.reshape(N, 8, 16, S, Q))
    j = np.where(rng.random((N, 8, 1, S, Q)) < 0.06, rng.integers(0, Q, (N, 8, 1, S, Q)), np.arange(Q))
    return np.take_along_axis(q, j, 4)
def pack(X, q, wv, kv):
    return {"x0": X.reshape(N, 128, W).astype(np.float32).astype(BF), "qs": np.ascontiguousarray(q).reshape(N, 128, S * Q).astype(np.float32).astype(BF),
            "wt": wv.reshape(N, 128, 1).astype(np.float32).astype(BF), "kk": np.repeat(kv, 16, axis=1).astype(np.int32)}
def setup_inputs(rng):
    wv, kv = hashes(rng); full = rng.random((N, 8)) < 0.5; bare = rng.choice(np.array([0.0, 0.002, 0.005, 0.02, 0.1]), (N, 8))
    full[:, 0] = True; bare[:, 0] = 0.0; bare[:, 1] = 0.005; bare[:, 2] = 0.02
    X = fill(rng, records(rng, 2 * W), wv, kv, full, bare)
    return pack(X, ask(rng, X, records(rng, S * Q)), wv, kv)
def setup_inputs_room(rng):
    wv, kv = hashes(rng); X = fill(rng, records(rng, 2 * W), wv, kv, np.ones((N, 8), bool), np.zeros((N, 8)))
    q = ask(rng, X, records(rng, S * Q)); pool = records(rng, 2 * Q); live, depth, path = search(X, pool, wv, kv)
    home = np.any(place(X, wv, kv) == np.arange(W)[:, None], axis=3)
    for r in range(N):
        for g in range(8):
            n = int(rng.choice(np.array([0, 1, C - 1, C, C + 1, Q])))
            if r == 0: n = (C, C + 1, Q, C - 1, 1, 0, C, Q)[g]
            used, take = set(), []
            for i in rng.permutation(2 * Q):
                p = set(path[r, g, i].tolist()) - {-1}
                if len(take) < n and live[r, g, i] and not (p & used):
                    take.append(int(i)); used |= p
            stay = rng.choice(np.nonzero(home[r, g])[0], Q - len(take))
            q[r, g, :, 0] = np.concatenate([pool[r, g][:, np.array(take, np.int64)], X[r, g][:, stay]], axis=1)[:, rng.permutation(Q)]
    return pack(X, q, wv, kv)
def setup_inputs_alike(rng):
    wv, kv = hashes(rng); wv[:] = wv[:1].copy(); kv[:, 2] = kv[:, 2, :1]; kv[:, 3, 1:] = kv[:, 3, 1:2]; kv[:] = kv[:1].copy()
    rec = (255 * rng.integers(0, 2, (N, 8, 16, 2 * W))).astype(np.int32); fresh = (255 * rng.integers(0, 2, (N, 8, 16, S * Q))).astype(np.int32)
    few = rng.integers(0, 256, (16, 24)).astype(np.int32)
    for g in (1, 5):
        for r in range(N):
            rec[r, g] = few[:, rng.integers(0, 24, 2 * W)]
            fresh[r, g] = np.where(rng.random(S * Q) < 0.5, few[:, rng.integers(0, 24, S * Q)], rng.integers(0, 256, (16, S * Q)))
    rec[:, 6, :, ::4] = 0
    rec[:, 7] = rng.integers(0, 3, (N, 16, 2 * W))
    full = rng.random((N, 8)) < 0.7; full[:, 1] = True; bare = rng.choice(np.array([0.0, 0.005, 0.02]), (N, 8))
    X = fill(rng, rec, wv, kv, full, bare); q = ask(rng, X, fresh)
    q[:, 4, :, 1] = q[:, 4, :, 1, :1]; q[:, 6, :, 2, ::5] = 0; q[:, 6, :, 0, Q - 1] = 255
    return pack(X, q, wv, kv)
def setup_inputs_hollow(rng):
    wv, kv = hashes(rng); bare = rng.choice(np.array([0.3, 0.6, 0.9, 0.97, 1.0]), (N, 8)); bare[0, 0] = 1.0; bare[1, 1] = 0.6
    full = rng.random((N, 8)) < 0.5; bare[:, 6:] = 0.0; full[:, 7] = True
    X = fill(rng, records(rng, 2 * W), wv, kv, full, bare); q = ask(rng, X, records(rng, S * Q))
    q[:, :, :, 2] = q[:, :, :, 1][..., rng.permutation(Q)]
    return pack(X, q, wv, kv)
def setup_inputs_edges(rng):
    wv, kv = hashes(rng); wv[:, 0] = 255; kv[:, :2] = rng.choice(np.array([1, 2046, 2047]), (N, 2, A)); kv[:, :2, 0] = 2047
    wv[:, 6, 0] |= 1; kv[:, 6] = kv[:, 6, :1].copy()
    full = rng.random((N, 8)) < 0.5; full[:, 0] = True; full[:, 4] = False; full[::2, 5] = True; full[1::2, 5] = False; full[:, 6] = False
    bare = np.zeros((N, 8)); bare[:, 3] = 0.3; bare[:, 7] = 0.1
    rec, fresh = records(rng, 2 * W), records(rng, S * Q)
    for v in (rec, fresh):
        k = v.shape[3]; v[:, 0] = np.where(rng.random((N, 1, k)) < 0.5, rng.integers(200, 256, (N, 16, k)), v[:, 0])
        v[::2, 5] = v[::2, 5] >> 2
    X = fill(rng, rec, wv, kv, full, bare); q = ask(rng, X, fresh)
    q[:, 0, :, 0, 0] = 255
    q[:, 1:3, :, 0, :8] = records(rng, 8)[:, 1:3]
    t = q[:, :, :, 0, :8].copy(); pl = place(t, wv, kv)[..., 0]; i = rng.integers(0, 16, (N, 8, 1, 8))
    near = np.where(np.arange(16)[:, None] == i, t + np.where(t < 255, 1, -1), t)
    for r in range(N):
        for g in (1, 2):
            for j in range(7, -1, -1): X[r, g, :, pl[r, g, j]] = near[r, g, :, j]
    X[:, 3] = np.where(rng.random((N, 1, W)) < 0.02, 0, X[:, 3]); X[:, 3, :, 0] = 512
    q[:, 3, :, 0, 0] = 0; q[:, 3, :, 1, 0] = 255
    X[:, 7, :, 0] = records(rng, 1)[:, 7, :, 0]; q[:, 7, :, 0, 0] = 0; pe = place(X[..., :1], wv, kv)[:, 7, 0]
    for r in range(N): X[r, 7, :, pe[r]] = 512
    for r in range(N):
        g = 4 + r % 2; c = rng.choice(np.nonzero(X[r, g, 0] != 512)[0], Q); q[r, g, :, 0] = X[r, g][:, c]
    q[1::2, 4, :, 0, 0] = records(rng, 1)[1::2, 4, :, 0]; q[1::2, 4, :, 1] = q[1::2, 4, :, 0, :1]
    rr = np.arange(8) % N; m = 256; pool = rng.integers(128, 256, (1, 8, 16, m)).astype(np.int32)
    live, depth, path = search(X[rr, 5][None], pool, wv[rr, 5][None], kv[rr, 5][None])
    for r in range(1, N, 2):
        p = path[0, r]; same = np.sum((p[:, None, :, None] == p[None, :, None, :]) & (p >= 0)[:, None, :, None], axis=(2, 3))
        fit = (same == 1) & live[0, r][:, None] & (live[0, r] & (depth[0, r] == L - 1))[None, :]
        a, b = divmod(int(np.argmax(fit)), m); z = pool[0, r][:, b:b + 1]
        q[r, 5, :, 1] = z; q[r, 5, :, 1, 0] = pool[0, r, :, a]
        X[r - 1, 5] = np.where(rng.random(W) < 0.125, z, X[r - 1, 5])
    mine = place(rec, wv, kv)[:, 6, :, 0]
    for r in range(1, N, 2):
        e = r - 1; p = mine[e]; i = np.nonzero(np.any(X[e, 6][:, p] != rec[e, 6], axis=0))[0]
        i = i[np.unique(p[i], return_index=True)[1]]
        t = place(X[e, 6][:, p[i]][None, None], wv[r:r + 1, 6:7], kv[r:r + 1, 6:7])[0, 0, :, 0]
        j = rng.permutation(np.unique(t, return_index=True)[1]); last = j[X[r, 6, 0, t[j]] != 512][:1]
        j = j[j != last[0]][:Q - 1]; j = np.concatenate([j[:C - 1], last, j[C - 1:]])
        q[e, 6] = rec[e, 6][:, i[j]][:, None, :]
        z = X[r, 6, :, int(t[last[0]])].copy()
        X[r, 6, :, t[j[:C]]] = 512
        c = rng.choice(np.nonzero(X[r, 6, 0] != 512)[0], S * Q); q[r, 6] = X[r, 6][:, c].reshape(16, S, Q); q[r, 6, :, 1, 0] = z
    return pack(X, q, wv, kv)
def setup_inputs_spread(rng):
    def uneven(k):
        v = np.minimum((np.exp2(2 + 6 * rng.random((N, 8, 1, k))) * rng.random((N, 8, 16, k))).astype(np.int32), 255)
        return np.where(rng.random((N, 8, 16, k)) < 0.02, 255, v).astype(np.int32)
    wv = np.minimum(np.exp2(8 * rng.random((N, 8, 16, 1))).astype(np.int32), 255); kv = np.minimum(np.exp2(11 * rng.random((N, 8, A))).astype(np.int64), 2047)
    X = fill(rng, uneven(2 * W), wv, kv, rng.random((N, 8)) < 0.6, rng.choice(np.array([0.0, 0.003, 0.01]), (N, 8)))
    return pack(X, ask(rng, X, uneven(S * Q)), wv, kv)
def check_inputs(d):
    bad = []
    v = np.asarray(d["x0"]).astype(np.float32); e = v == 512
    if not np.all(e | ((v >= 0) & (v <= 255) & (np.floor(v) == v))): bad.append("range of x0")
    e = e.reshape(N, 8, 16, W)
    if np.any(np.any(e, axis=2) != np.all(e, axis=2)): bad.append("empty records of x0")
    for k, lo in (("qs", 0), ("wt", 1)):
        v = np.asarray(d[k]).astype(np.float32)
        if not np.all((v >= lo) & (v <= 255) & (np.floor(v) == v)): bad.append("range of " + k)
    k = np.asarray(d["kk"])
    if np.min(k) < 1 or np.max(k) > 2047: bad.append("range of kk")
    k = k.reshape(N, 8, 16, A)
    if np.any(k != k[:, :, :1]): bad.append("rows of kk")
    return bad
def reference(x0, qs, wt, kk):
    X = x0.astype(np.float32).astype(np.int32).reshape(N, 8, 16, W); q = qs.astype(np.float32).astype(np.int32).reshape(N, 8, 16, S, Q)
    wv = wt.astype(np.float32).astype(np.int32).reshape(N, 8, 16, 1); kv = kk.reshape(N, 8, 16, A)[:, :, 0].astype(np.int64)
    come = np.full((N, 8, 16, C), 512, np.int32)
    for s in range(S):
        X, out = step(X, np.concatenate([q[:, :, :, s], come], axis=3), wv, kv)
        come = np.roll(out, 1, axis=0)
    return {"y": X.reshape(N, 128, W).astype(np.float32).astype(BF)}

@@ -1,0 +1,491 @@
+from concourse.mybir import AluOpType, AxisListType, ActivationFunctionType
+
+A = AluOpType
+ACT = ActivationFunctionType
+X = AxisListType.X
+S = 5
+E11 = 2048.0
+OFFS = -8388608.0
+PEN = -33554432.0
+BASE = (96, 384, 1536)
+ORDER = "d0 s0 lc rq k3 x1 m0 d1 r2 s1 k1 m1 d2 s2 fe r3 fq k2 m2 d3 s3 m3 g6 x6 fa d4 s4 m4 m6 d5 s5 m5 p12 d7 s7 m7 fp fg pp lv r12 pg"
+
+SCRATCH = {}
+for _t, _l in (
+        ("bfloat16", "XB:2432 QS:480 WTS:1 MT:128 MT2:128 ML:128 IO16:384 EK:2048 WR:2048 WBD:128 ONE:512 IB:128 NIB:128 IPEN:128"
+                     " IOFF:128 BDB:128 LTB:128 MKB:128 OCC1:512 OCC2:2048 OCC3:2048 AB1:512 AB2:2048 DF:8192 FE1:32 FQ2:128"
+                     " FA:128 FB:128 FP:512 FG:512 OLD:512 ND:8 SB0:256 SB1:256 SB2:256 SB3:256 ARR1:32 ARR2:32 ARR3:32 ARR4:32"),
+        ("float32", "KF:4 KG:4 KH:4 K32:4 MASK:384 PMF:1 LN0:8 LN:8 TRC:24 TRD:24 TL:8 IX3F:512 RS:32 RQ:2 RE:32 RF:2 LV:8 LIVE:8 NEQ:8"
+                    " M12:8 M3:8 MF:8 OWNF:24 CFM:8 GB:8 GO:8 W1:24 W2:24 W3:24 NE:8 D2:8 D3:8"),
+        ("float16", "IH:128 BDH:128 NTL:8 IX3:512 SELM:384"),
+        ("int32", "KKI:4 PIN:1 PMI:1 BH:8 PLW:2048 P1A:120 P1R:128 UI:128 U:128 Z:512 Y:512 MI:8 PG:8 PO:24"),
+        ("uint16", "OF:672 L1U:120 POU:24 XL:24 DLU:24 SLU:8")):
+    for _w in _l.split():
+        SCRATCH[_w.split(":")[0]] = ("sbuf", [128, int(_w.split(":")[1])], _t)
+for _n, _s, _t in (("QR", [128, 30, 1024], "bfloat16"), ("QRR", [128, 2, 512], "bfloat16"), ("IX12F", [128, 8, 20], "float32"),
+                   ("IX12", [128, 8, 20], "float16"), ("NH", [128, 8, 4], "float32"), ("N1", [128, 8, 2], "float32"),
+                   ("OTHH", [128, 3, 128], "float16"), ("EQ", [128, 72, 128], "bfloat16")):
+    SCRATCH[_n] = ("sbuf", _s, _t)
+BANKS = ("SD", "SR", "K12", "K3", "DA", "DB", "OT", "OW")
+for _n, _s in (("SD", [128, 128]), ("SR", [128, 128]), ("K12", [128, 8, 20]), ("K3", [128, 512]), ("DA", [128, 512]), ("DB", [128, 512]),
+               ("OT", [128, 384]), ("OW", [128, 64])):
+    SCRATCH[_n] = ("psum", _s, "float32")
+SEMAPHORES = ["cv", "cs", "cp", "cg", "sent"] + ["arr%d" % (i + 1) for i in range(S - 1)] + ["d%d" % i for i in range(40)]
+
+
+def make_queue(g, T):
+    eng = {"v": g.vector, "s": g.scalar, "p": g.tensor, "g": g, "y": g.sync}
+    count = {"cv": 0, "cs": 0, "cp": 0, "cg": 0}
+    known = {q: {} for q in eng}
+    snap, writer, readers, touch = {}, {}, {}, {}
+    dmas = [0]
+
+    def before(q, rd, wr):
+        evs = []
+        for t in rd:
+            if t in BANKS:
+                evs += [e for e in touch.get(t, {}).values() if e[2] != q]
+            elif t in writer:
+                evs.append(writer[t])
+        for t in wr:
+            if t in BANKS:
+                evs += [e for e in touch.get(t, {}).values() if e[2] != q]
+            elif readers.get(t):
+                evs += list(readers[t].values()) + ([writer[t]] if t in writer else [])
+            elif t in writer and writer[t][2] != q:
+                evs.append(writer[t])
+        best = {}
+        for sem, val, _ in evs:
+            best[sem] = max(best.get(sem, 0), val)
+        for sem in sorted(best):
+            val = best[sem]
+            if known[q].get(sem, 0) < val:
+                eng[q].wait_ge(T.sem[sem], val)
+                for k, n in snap.get((sem, val), {}).items():
+                    known[q][k] = max(known[q].get(k, 0), n)
+                known[q][sem] = val
+
+    def after(ev, rd, wr):
+        for t in rd:
+            if t in BANKS:
+                touch.setdefault(t, {})[ev[2]] = ev
+            else:
+                readers.setdefault(t, {})[(ev[2], ev[0])] = ev
+        for t in wr:
+            if t in BANKS:
+                touch.setdefault(t, {})[ev[2]] = ev
+            else:
+                writer[t] = ev
+                readers[t] = {}
+
+    def op(q, rd, wr, call):
+        before(q, rd, wr)
+        sem = "c" + q
+        count[sem] += 1
+        call(eng[q]).then_inc(T.sem[sem], 1)
+        snap[(sem, count[sem])] = dict(known[q])
+        after((sem, count[sem], q), rd, wr)
+
+    def dma(q, rd, wr, out, in_):
+        before(q, rd, wr)
+        sem = "d%d" % dmas[0]
+        dmas[0] += 1
+        eng[q].dma_start(out, in_).then_inc(T.sem[sem], 16)
+        snap[(sem, 16)] = dict(known[q])
+        after((sem, 16, "dma"), rd, wr)
+
+    def outside(sem, val, wr):
+        after((sem, val, "far"), [], wr)
+
+    def finish():
+        for sem in ("cv", "cs", "cp", "cg"):
+            if known["g"].get(sem, 0) < count[sem]:
+                g.wait_ge(T.sem[sem], count[sem])
+        for i in range(dmas[0]):
+            g.wait_ge(T.sem["d%d" % i], 16)
+    return op, dma, outside, before, finish
+
+
+def rank_program(g, core, T, topo):
+    rank = T.rank_of(core)
+    if rank is None:
+        return
+    op, dma, outside, before, finish = make_queue(g, T)
+    nxt = T.cores[(rank + 1) % len(T.cores)]
+    rid, pid = topo.addr(nxt, core)
+    wire = topo.mask(core, nxt)
+    nwire = len(topo.engines(core, nxt))
+    nland = len(topo.engines(T.cores[(rank - 1) % len(T.cores)], core))
+
+    dma("y", [], ["QS"], T.QS[:], T.qs[:])
+    dma("s", [], ["WTS"], T.WTS[:], T.wt[:])
+    dma("s", [], ["KKI"], T.KKI[:], T.kk[:])
+    dma("y", [], ["QR0"], T.QR[:, 0:6, 0:16], T.qs[:, 0:96])
+    dma("s", [], ["XBx"], T.XB[:, 256:1280], T.x0[:, 0:1024])
+    dma("y", [], ["XBx2"], T.XB[:, 1280:2304], T.x0[:, 1024:2048])
+    for s in range(1, S):
+        dma("y", [], ["QR%d" % s], T.QR[:, 6 * s:6 * s + 6, 0:16], T.qs[:, 96 * s:96 * s + 96])
+    dma("y", [], ["XBqD"], T.XB[:, 0:96], T.qs[:, 0:96])
+    dma("y", [], ["OLDqD"], T.OLD[:, 384:480], T.qs[:, 0:96])
+
+    def iota(tok, out, pattern, base, cm, small=True):
+        if small:
+            op("g", [], [tok], lambda e: e.iota(out, pattern, base, cm, allow_small_or_imprecise_dtypes=True))
+        else:
+            op("g", [], [tok], lambda e: e.iota(out, pattern, base, cm))
+
+    def sel(rd, tok, out, in_, pattern, cmp, fill, base, cm):
+        op("g", [rd], [tok], lambda e: e.affine_select(out, in_, pattern, cmp, fill, base, cm))
+
+    def vset(tok, out, c):
+        op("v", [], [tok], lambda e: e.memset(out, c))
+
+    def ts(rd, wr, out, in0, s1, s2, op0, op1=None):
+        if op1 is None:
+            op("v", rd, wr, lambda e: e.tensor_scalar(out, in0, s1, None, op0=op0))
+        else:
+            op("v", rd, wr, lambda e: e.tensor_scalar(out, in0, s1, s2, op0=op0, op1=op1))
+
+    def tt(rd, wr, out, a, b, o):
+        op("v", rd, wr, lambda e: e.tensor_tensor(out, a, b, o))
+
+    def cp(rd, wr, out, a):
+        op("v", rd, wr, lambda e: e.tensor_copy(out, a))
+
+    def red(rd, wr, out, a, o):
+        op("v", rd, wr, lambda e: e.tensor_reduce(out, a, X, o))
+
+    def act(rd, wr, out, a, func):
+        op("s", rd, wr, lambda e: e.activation(out, a, func))
+
+    def mm(rd, bank, out, lhsT, rhs, start, stop):
+        op("p", rd, [bank], lambda e: e.matmul(out, lhsT, rhs, start, stop))
+
+    iota("MT", T.MT[:], [[0, 8], [1, 16]], 0, 0)
+    sel("MT", "MT2", T.MT2[:], T.MT[:], [[-16, 8], [0, 16]], A.is_ge, -1.0, 0, 1)
+    sel("MT2", "ML", T.ML[:], T.MT2[:], [[16, 8], [0, 16]], A.is_ge, -1.0, 15, -1)
+    vset("ONE", T.ONE[:], 1.0)
+    sel("ONE", "IB", T.IB[:], T.ONE[:, 0:128], [[-1, 128]], A.is_equal, 0.0, 0, 1)
+    iota("PIN", T.PIN[:], [[0, 1]], 0, 1, False)
+    iota("IO16", T.IO16[:], [[0, 24], [1, 16]], 0, 0)
+    iota("LN0", T.LN0[:], [[16, 8]], 0, 0)
+    iota("BH", T.BH[:], [[1, 8]], 8, 0, False)
+    iota("IX12F", T.IX12F[:, :, 0:4], [[4, 8], [1, 4]], BASE[0], 0)
+    iota("IX12F", T.IX12F[:, :, 4:20], [[16, 8], [1, 16]], BASE[1], 0)
+    iota("IX3F", T.IX3F[:], [[1, 512]], BASE[2], 0)
+    op("v", [], ["XBq", "XBt"], lambda e: e.memset(T.XB[:, 96:256], 0.0))
+    vset("XBt2", T.XB[:, 2304:2432], 0.0)
+    vset("PLW0", T.PLW[:], -256)
+    vset("NH", T.NH[:], 0.0)
+    vset("M12", T.M12[:], OFFS)
+    vset("M3", T.M3[:], OFFS)
+    vset("NEQ", T.NEQ[:], 1.0)
+    for r in range(16):
+        ts(["ML", "WTS"], ["WR"], T.WR[:, 128 * r:128 * r + 128], T.ML[:], float(r), T.WTS[:, 0:1], A.is_equal, A.mult)
+    cp(["KKI"], ["KF"], T.KF[:], T.KKI[:])
+    ts(["KF"], ["KG"], T.KG[:], T.KF[:], 1024.0, -2048.0, A.is_gt, A.mult)
+    tt(["KF", "KG"], ["KH"], T.KH[:], T.KF[:], T.KG[:], A.add)
+    ts(["KH"], ["K32"], T.K32[:], T.KH[:], 32.0, None, A.mult)
+
+    def places(rd, src, n, dst, dtok):
+        cp(rd, ["UI"], T.UI[:, 0:n], src)
+        ts(["UI"], ["U"], T.U[:, 0:n], T.UI[:, 0:n], 2047, None, A.bitwise_and)
+        for a in range(4):
+            ts(["U", "K32"], ["Z%d" % a], T.Z[:, a * n:a * n + n], T.U[:, 0:n], T.K32[:, a:a + 1], None, A.add)
+        for a in range(4):
+            tt(["Z%d" % a, "U"], ["Y"], T.Y[:, a:4 * n:4], T.Z[:, a * n:a * n + n], T.U[:, 0:n], A.mult)
+        ts(["Y"], [dtok], dst, T.Y[:, 0:4 * n], 5, 2047, A.arith_shift_right, A.bitwise_and)
+
+    def wrapsum(mat, rd, bank, out, rhs, start, stop):
+        for r in range(16):
+            mm([mat] + rd, bank, out, T[mat][:, 128 * r:128 * r + 128], rhs(r), start and r == 0, stop and r == 15)
+
+    wrapsum("WR", ["QS"], "SD", T.SD[:, 0:30], lambda r: T.QS[:, r:480:16], True, True)
+    for r in range(16):
+        ts(["ML"], ["EK"], T.EK[:, 128 * r:128 * r + 128], T.ML[:], float(r), E11, A.is_equal, A.mult)
+    places(["SD"], T.SD[:, 0:30], 30, T.P1A[:], "P1A")
+    cp(["P1A"], ["L1U"], T.L1U[:], T.P1A[:])
+    w = 16
+    while w < 512:
+        act(["QR0"], ["QR0"], T.QR[:, 0:6, w:2 * w], T.QR[:, 0:6, 0:w], ACT.Copy)
+        w *= 2
+    dma("y", ["QR0"], ["QX0"], T.QR[:, 0:6, 512:1024], T.QR[:, 0:6, 0:512])
+    ts(["IB"], ["NIB"], T.NIB[:], T.IB[:], -1.0, None, A.mult)
+    ts(["IB"], ["IPEN"], T.IPEN[:], T.IB[:], PEN, None, A.mult)
+    ts(["IB"], ["IOFF"], T.IOFF[:], T.IB[:], OFFS, None, A.mult)
+    cp(["IX12F"], ["IX12"], T.IX12[:], T.IX12F[:])
+    cp(["IX3F"], ["IX3"], T.IX3[:], T.IX3F[:])
+    cp(["IB"], ["IH"], T.IH[:], T.IB[:])
+    ts(["ML"], ["BDB"], T.BDB[:], T.ML[:], 0.0, None, A.is_ge)
+    ts(["ML"], ["BDH"], T.BDH[:], T.ML[:], 0.0, None, A.is_ge)
+    ts(["ML", "WTS"], ["WBD"], T.WBD[:], T.ML[:], 0.0, T.WTS[:, 0:1], A.is_ge, A.mult)
+    ts(["PIN"], ["PMI"], T.PMI[:], T.PIN[:], 15, None, A.bitwise_and)
+    cp(["PMI"], ["PMF"], T.PMF[:], T.PMI[:])
+    ts(["LN0", "PMF"], ["LN"], T.LN[:], T.LN0[:], T.PMF[:, 0:1], None, A.add)
+    ts(["LN", "PLW0"], ["PLWA"], T.PLW[:, 24:32], T.LN[:], -256.0, None, A.add)
+    ts(["LN", "PLW0"], ["PLWB"], T.PLW[:, 8:16], T.LN[:], -128.0, None, A.add)
+    sel("BDB", "LTB", T.LTB[:], T.BDB[:], [[1, 128]], A.is_gt, 0.0, 0, -1)
+    XR = ["XBx", "XBx2"]
+
+    def gather(q, rd, wr, out, lst):
+        if q == "v":
+            cp(rd + XR, wr, out, T.XB[:, 256:2304].indirect(lst))
+        else:
+            act(rd + XR, wr, out, T.XB[:, 256:2304].indirect(lst), ACT.Copy)
+
+    diffs = [0]
+
+    def diff(rd, rt, occ, reps, n, out, otok):
+        bank = ("DA", "DB")[diffs[0] % 2]
+        diffs[0] += 1
+        ps = T[bank][:, 0:n]
+        mm(["IB"] + rd, bank, ps, T.IB[:], occ, True, False)
+        mm(["NIB", rt], bank, ps, T.NIB[:], reps, False, True)
+        act([bank], [otok], out, ps, ACT.Abs)
+
+    for s in range(S):
+        arrivals = s > 0
+        H = 8 if arrivals else 6
+        both = ("D", "R") if arrivals else ("D",)
+        at, qt = "ARR%d" % s, "QR%d" % s
+        arr = T[at] if arrivals else None
+        PL1, PL2, PL3 = (["PLW%d%s" % (l, b) for b in both] for l in (1, 2, 3))
+        if arrivals:
+            outside("arr%d" % s, nland, [at])
+            dma("y", [], ["XBqD"], T.XB[:, 0:96], T.qs[:, 96 * s:96 * s + 96])
+            dma("y", [], ["OLDqD"], T.OLD[:, 384:480], T.qs[:, 96 * s:96 * s + 96])
+
+        gather("s", ["L1U"], ["OCC1D"], T.OCC1[:, 0:384], T.L1U[:, 24 * s:24 * s + 24])
+        cp(["P1A"], ["PLW1D"], T.PLW[:, 96:120], T.P1A[:, 24 * s:24 * s + 24])
+        wrapsum("WR", ["OCC1D"], "SD", T.SD[:, 0:24], lambda r: T.OCC1[:, r:384:16], True, True)
+        diff(["OCC1D"], qt, T.OCC1[:, 0:384], T.QR[:, 6 * s:6 * s + 6, 0:64], 384, T.AB1[:, 0:384], "AB1D")
+        places(["SD"], T.SD[:, 0:24], 24, T.PLW[:, 384:480], "PLW2D")
+        cp(["PLW2D"], ["OF2D"], T.OF[:, 32:128], T.PLW[:, 384:480])
+        gather("s", ["OF2D"], ["OCC2Ds"], T.OCC2[:, 0:768], T.OF[:, 32:80])
+        gather("v", ["OF2D"], ["OCC2Dv"], T.OCC2[:, 768:1536], T.OF[:, 80:128])
+        wrapsum("WR", ["OCC2Ds", "OCC2Dv"], "SD", T.SD[:, 32:128], lambda r: T.OCC2[:, r:1536:16], True, True)
+        for c in range(3):
+            diff((["OCC2Ds"], ["OCC2Ds", "OCC2Dv"], ["OCC2Dv"])[c], qt, T.OCC2[:, 512 * c:512 * c + 512],
+                 T.QR[:, 6 * s + 2 * c:6 * s + 2 * c + 2, 0:256], 512, T.AB2[:, 512 * c:512 * c + 512], "AB2%d" % c)
+        places(["SD"], T.SD[:, 32:128], 96, T.PLW[:, 1536:1920], "PLW3D")
+        cp(["PLW3D"], ["OF3D"], T.OF[:, 160:544], T.PLW[:, 1536:1920])
+
+        if arrivals:
+            for k in range(2):
+                sel(at, "QRR", T.QRR[:, k, 0:16], arr[:, 16 * k:16 * k + 16], [[0, 16]], A.is_equal, 0.0, 0, 0)
+            w = 16
+            while w < 512:
+                sel("QRR", "QRR", T.QRR[:, :, w:2 * w], T.QRR[:, :, 0:w], [[0, 2], [0, w]], A.is_equal, 0.0, 0, 0)
+                w *= 2
+            dma("y", [at], ["XBqR"], T.XB[:, 96:128], arr[:])
+            dma("y", [at], ["OLDqR"], T.OLD[:, 480:512], arr[:])
+        if s + 1 < S:
+            w, nt, lo = 16, "QR%d" % (s + 1), 6 * (s + 1)
+            while w < 512:
+                sel(nt, nt, T.QR[:, lo:lo + 6, w:2 * w], T.QR[:, lo:lo + 6, 0:w], [[0, 6], [0, w]], A.is_equal, 0.0, 0, 0)
+                w *= 2
+            dma("y", [nt], ["QX%d" % (s + 1)], T.QR[:, lo:lo + 6, 512:1024], T.QR[:, lo:lo + 6, 0:512])
+
+        def df(hi):
+            return T.DF[:, 1024 * hi:1024 * hi + 1024]
+
+        def p_d(hi):
+            if hi < 6:
+                tt(["OF3D", qt, "QX%d" % s] + XR, ["DF%d" % hi], df(hi),
+                   T.XB[:, 256:2304].indirect(T.OF[:, 160 + 64 * hi:224 + 64 * hi]), T.QR[:, 6 * s + hi, :], A.subtract)
+            else:
+                for c in range(2):
+                    o, l = 1024 * hi + 512 * c, 160 + 64 * hi + 32 * c
+                    tt(["OF3R", "QRR"] + XR, ["DF%d" % hi], T.DF[:, o:o + 512],
+                       T.XB[:, 256:2304].indirect(T.OF[:, l:l + 32]), T.QRR[:, hi - 6, :], A.subtract)
+
+        def p_s(hi):
+            act(["DF%d" % hi], ["DF%d" % hi], df(hi), df(hi), ACT.Abs)
+
+        def p_m(hi):
+            wrapsum("EK", ["DF%d" % hi], "K3", T.K3[:, 64 * hi:64 * hi + 64], lambda r: T.DF[:, 1024 * hi + r:1024 * hi + 1024:16], False, False)
+
+        def p_g(hi):
+            k = hi - 6
+            gather("s", ["OF3R"], ["OCC3%d" % k], T.OCC3[:, 1024 * k:1024 * k + 1024], T.OF[:, 544 + 64 * k:608 + 64 * k])
+
+        def p_x(hi):
+            if hi == 1:
+                diff(["OCC1R"], "QRR", T.OCC1[:, 384:512], T.QRR[:, :, 0:64], 128, T.AB1[:, 384:512], "AB1R")
+                return
+            k = hi - 6
+            for c in range(2):
+                o = 1024 * k + 512 * c
+                diff(["OCC3%d" % k], "QRR", T.OCC3[:, o:o + 512], T.QRR[:, k, :], 512, T.DF[:, 6144 + o:6144 + o + 512], "DF%d" % hi)
+
+        def p_rq():
+            mm(["WBD", at], "SR", T.SR[:, 0:32], T.WBD[:], arr[:], True, True)
+            tt(["MASK", "SR"], ["RS"], T.RS[:], T.SR[:, 0:32], T.MASK[:, 0:32], A.mult)
+            tt(["MASK", at], ["RE"], T.RE[:], arr[:], T.MASK[:, 0:32], A.mult)
+            for k in range(2):
+                red(["RS"], ["RQ"], T.RQ[:, k:k + 1], T.RS[:, 16 * k:16 * k + 16], A.add)
+            places(["RQ"], T.RQ[:], 2, T.PLW[:, 120:128], "PLW1R")
+            cp(["PLW1R"], ["OF1R"], T.OF[:, 24:32], T.PLW[:, 120:128])
+            gather("s", ["OF1R"], ["OCC1R"], T.OCC1[:, 384:512], T.OF[:, 24:32])
+            wrapsum("WR", ["OCC1R"], "SR", T.SR[:, 32:40], lambda r: T.OCC1[:, 384 + r:512:16], True, True)
+            for k in range(2):
+                red(["RE"], ["RF"], T.RF[:, k:k + 1], T.RE[:, 16 * k:16 * k + 16], A.add)
+            ts(["RF"], ["NEQ"], T.NEQ[:, 6:8], T.RF[:], 512.0, None, A.is_lt)
+
+        def p_r2():
+            places(["SR"], T.SR[:, 32:40], 8, T.PLW[:, 480:512], "PLW2R")
+            cp(["PLW2R"], ["OF2R"], T.OF[:, 128:160], T.PLW[:, 480:512])
+            gather("s", ["OF2R"], ["OCC2R"], T.OCC2[:, 1536:2048], T.OF[:, 128:160])
+            wrapsum("WR", ["OCC2R"], "SR", T.SR[:, 64:96], lambda r: T.OCC2[:, 1536 + r:2048:16], True, True)
+            diff(["OCC2R"], "QRR", T.OCC2[:, 1536:2048], T.QRR[:, :, 0:256], 512, T.AB2[:, 1536:2048], "AB23")
+
+        def p_r3():
+            places(["SR"], T.SR[:, 64:96], 32, T.PLW[:, 1920:2048], "PLW3R")
+            cp(["PLW3R"], ["OF3R"], T.OF[:, 544:672], T.PLW[:, 1920:2048])
+
+        def p_lc():
+            ts(["IO16", "PMF"], ["MASK"], T.MASK[:], T.IO16[:], T.PMF[:, 0:1], None, A.is_equal)
+            for t, c in enumerate((0.0, 128.0, 2304.0)):
+                ts(["LN"], ["TRC"], T.TRC[:, 8 * t:8 * t + 8], T.LN[:], c, None, A.add)
+                ts(["LN"], ["TRD"], T.TRD[:, 8 * t:8 * t + 8], T.LN[:], -1.0, 256.0 - c, A.mult, A.add)
+            ts(["LN"], ["TL"], T.TL[:], T.LN[:], 128.0, None, A.add)
+            ts(["TL"], ["NTL"], T.NTL[:], T.TL[:], -1.0, None, A.mult)
+            vset("MKB", T.MKB[:, 0:112], 0.0)
+            ts(["IO16", "PMF"], ["MKB"], T.MKB[:, 112:128], T.IO16[:, 0:16], T.PMF[:, 0:1], -16.0, A.is_ge, A.mult)
+            for i in range(S - 1):
+                vset("SB%d" % i, T["SB%d" % i][:], 512.0)
+            vset("OLDqR", T.OLD[:, 480:512], 0.0)
+
+        def p_k3():
+            mm(["IOFF", "ONE"], "K3", T.K3[:, 0:64 * H], T.IOFF[:], T.ONE[:, 0:64 * H], True, False)
+            mm(["IH", "IX3"], "K3", T.K3[:, 0:64 * H], T.IH[:], T.IX3[:, 0:64 * H], False, False)
+
+        def p_k1():
+            mm(["IOFF", "ONE"], "K12", T.K12[:, 0:H, 0:4], T.IOFF[:], T.ONE[:, 0:4 * H], True, False)
+            mm(["IH", "IX12"], "K12", T.K12[:, 0:H, 0:4], T.IH[:], T.IX12[:, 0:H, 0:4], False, False)
+            wrapsum("EK", ["AB1" + b for b in both], "K12", T.K12[:, 0:H, 0:4], lambda r: T.AB1[:, r:64 * H:16], False, True)
+
+        def p_fe():
+            ts(["K12"], ["FE1"], T.FE1[:, 0:4 * H], T.K12[:, 0:H, 0:4], 0.0, None, A.is_ge)
+            ts(["K12"], ["NH"], T.NH[:, 0:H, :], T.K12[:, 0:H, 0:4], OFFS + E11, None, A.is_ge)
+
+        def p_fq():
+            for a in range(4):
+                tt(PL2 + PL1, ["FQ2"], T.FQ2[:, a:16 * H:4], T.PLW[:, 384 + a:384 + 16 * H:4], T.PLW[:, 96:96 + 4 * H], A.is_equal)
+
+        def p_k2():
+            mm(["IOFF", "ONE"], "K12", T.K12[:, 0:H, 4:20], T.IOFF[:], T.ONE[:, 0:16 * H], True, False)
+            mm(["IH", "IX12"], "K12", T.K12[:, 0:H, 4:20], T.IH[:], T.IX12[:, 0:H, 4:20], False, False)
+            wrapsum("EK", ["AB2%d" % i for i in range(H // 2)], "K12", T.K12[:, 0:H, 4:20], lambda r: T.AB2[:, r:256 * H:16], False, False)
+            for a in range(4):
+                mm(["IPEN", "FE1"], "K12", T.K12[:, 0:H, 4 + a:20:4], T.IPEN[:], T.FE1[:, 0:4 * H], False, False)
+            mm(["IPEN", "FQ2"], "K12", T.K12[:, 0:H, 4:20], T.IPEN[:], T.FQ2[:, 0:16 * H], False, True)
+
+        def p_fa():
+            for f, c, o in (("FA", 0.0, A.is_ge), ("FB", OFFS, A.is_lt)):
+                ts(["K12"], [f], T[f][:, 0:16 * H], T.K12[:, 0:H, 4:20], c, None, o)
+
+        def p_p12():
+            for a in range(4):
+                for f in ("FA", "FB"):
+                    mm(["IPEN", f], "K3", T.K3[:, a:64 * H:4], T.IPEN[:], T[f][:, 0:16 * H], False, False)
+
+        def p_fp():
+            for a in range(4):
+                tt(PL3 + PL2, ["FP"], T.FP[:, a:64 * H:4], T.PLW[:, 1536 + a:1536 + 64 * H:4], T.PLW[:, 384:384 + 16 * H], A.is_equal)
+
+        def p_fg():
+            for a in range(4):
+                cp(PL1, ["P1R"], T.P1R[:, a:16 * H:4], T.PLW[:, 96:96 + 4 * H])
+            for a in range(4):
+                tt(PL3 + ["P1R"], ["FG"], T.FG[:, a:64 * H:4], T.PLW[:, 1536 + a:1536 + 64 * H:4], T.P1R[:, 0:16 * H], A.is_equal)
+
+        def p_pp():
+            mm(["IPEN", "FP"], "K3", T.K3[:, 0:64 * H], T.IPEN[:], T.FP[:, 0:64 * H], False, False)
+
+        def p_pg():
+            mm(["IPEN", "FG"], "K3", T.K3[:, 0:64 * H], T.IPEN[:], T.FG[:, 0:64 * H], False, True)
+
+        def p_lv():
+            tt(["NH"], ["N1"], T.N1[:], T.NH[:, :, 0:2], T.NH[:, :, 2:4], A.mult)
+            tt(["N1"], ["LV"], T.LV[:], T.N1[:, :, 0], T.N1[:, :, 1], A.mult)
+            tt(["LV", "NEQ"], ["LIVE"], T.LIVE[:], T.LV[:], T.NEQ[:], A.mult)
+
+        def p_r12():
+            for hi in range(H):
+                red(["K12"], ["M12"], T.M12[:, hi:hi + 1], T.K12[:, hi, :], A.max)
+
+        by_block = {"d": p_d, "s": p_s, "m": p_m, "g": p_g, "x": p_x}
+        whole = {"rq": p_rq, "r2": p_r2, "r3": p_r3, "lc": p_lc, "k3": p_k3, "k1": p_k1, "fe": p_fe, "fq": p_fq, "k2": p_k2, "fa": p_fa,
+                 "p12": p_p12, "fp": p_fp, "fg": p_fg, "pp": p_pp, "pg": p_pg, "lv": p_lv, "r12": p_r12}
+        for w in ORDER.split():
+            if w == "lc" and s > 0 or not arrivals and (w[0] == "r" and w != "r12" or w in ("x1", "d6", "s6", "m6", "g6", "x6", "d7", "s7", "m7", "g7", "x7")):
+                continue
+            if w in whole:
+                whole[w]()
+            else:
+                by_block[w[0]](int(w[1:]))
+
+        for hi in range(H):
+            red(["K3"], ["M3"], T.M3[:, hi:hi + 1], T.K3[:, 64 * hi:64 * hi + 64], A.max)
+        tt(["M12", "M3"], ["MF"], T.MF[:], T.M12[:], T.M3[:], A.max)
+        tt(["MF", "LIVE"], ["MI"], T.MI[:], T.MF[:], T.LIVE[:], A.mult)
+        ts(["MI"], ["PG"], T.PG[:], T.MI[:], 4, 127, A.arith_shift_right, A.bitwise_and)
+        ts(["MI"], ["PO"], T.PO[:, 0:8], T.MI[:], 2047, None, A.bitwise_and)
+        ts(["MI"], ["PO"], T.PO[:, 8:16], T.MI[:], 2, 511, A.arith_shift_right, A.bitwise_and)
+        tt(["PG", "BH"], ["PO"], T.PO[:, 16:24], T.PG[:], T.BH[:], A.max)
+        cp(["PO"], ["POU"], T.POU[:], T.PO[:])
+        ts(["MF"], ["NE"], T.NE[:], T.MF[:], 0.0, None, A.is_lt)
+        tt(["POU", "MASK", "PLW0", "PLWA", "PLWB"] + PL1 + PL2 + PL3, ["SELM"],
+           T.SELM[:], T.PLW[:, 0:2048].indirect(T.POU[:, 0:24]), T.MASK[:], A.mult)
+        mm(["BDH", "SELM"], "OT", T.OT[:], T.BDH[:], T.SELM[:], True, True)
+        for r in range(16):
+            mm(["IH", "SELM"], "OW", T.OW[:, 0:24], T.IH[:], T.SELM[:, r:384:16], r == 0, r == 15)
+        cp(["OT"], ["OTHH"], T.OTHH[:], T.OT[:])
+        act(["OW"], ["OWNF"], T.OWNF[:], T.OW[:, 0:24], ACT.Copy)
+        ts(["OWNF"], ["XL"], T.XL[:], T.OWNF[:], 256.0, None, A.add)
+        xall = XR + ["XBqD", "XBqR", "XBq", "XBt", "XBt2"]
+        act(["XL"] + xall, ["OLD"], T.OLD[:, 0:384], T.XB[:, 0:2432].indirect(T.XL[:, 0:24]), ACT.Copy)
+        for hi in range(7, -1, -1):
+            n = 16 * (hi + 1)
+            bank, o = ("DA", 8 * hi * (hi + 1)) if hi < 6 else ("DB", 112 * (hi - 6))
+            out = T[bank][:, o:o + n]
+            mm(["IB", "MKB"], bank, out, T.IB[:], T.MKB[:, 128 - n:128], True, False)
+            for t in range(3):
+                k = 3 * (3 * hi + t)
+                ts(["OTHH", "OWNF"], ["EQ%d" % k], T.EQ[:, k:k + 3, 0:n], T.OTHH[:, :, 0:n],
+                   T.OWNF[:, 8 * t + hi:8 * t + hi + 1], None, A.is_equal)
+                for t2 in range(3):
+                    mm(["IB", "EQ%d" % k], bank, out, T.IB[:], T.EQ[:, k + t2, 0:n], False, t == 2 and t2 == 2)
+        tt(["OWNF", "TRD"], ["W1"], T.W1[:], T.OWNF[:], T.TRD[:], A.add)
+        for hi in range(7, -1, -1):
+            n = 16 * (hi + 1)
+            bank, o = ("DA", 8 * hi * (hi + 1)) if hi < 6 else ("DB", 112 * (hi - 6))
+            red([bank], ["CFM"], T.CFM[:, hi:hi + 1], T[bank][:, o:o + n], A.max)
+        ts(["CFM"], ["GB"], T.GB[:], T.CFM[:], 0.5, None, A.is_lt)
+        tt(["GB", "LIVE"], ["GO"], T.GO[:], T.GB[:], T.LIVE[:], A.mult)
+        send = s + 1 < S
+        if send:
+            tt(["GO", "NE"], ["ND"], T.ND[:], T.GO[:], T.NE[:], A.mult)
+            mm(["IH", "NTL"], "OW", T.OW[:, 32:40], T.IH[:], T.NTL[:], True, False)
+            mm(["LTB", "ND"], "OW", T.OW[:, 32:40], T.LTB[:], T.ND[:], False, False)
+            for d in range(1, 8):
+                mm(["BDB", "ND"], "OW", T.OW[:, 32 + d:40], T.BDB[:], T.ND[:, 0:8 - d], False, d == 7)
+        for t in range(3):
+            tt(["GO", "W1"], ["W2"], T.W2[:, 8 * t:8 * t + 8], T.W1[:, 8 * t:8 * t + 8], T.GO[:], A.mult)
+        tt(["W2", "TRC"], ["W3"], T.W3[:], T.W2[:], T.TRC[:], A.add)
+        cp(["W3"], ["DLU"], T.DLU[:], T.W3[:])
+        op("v", ["DLU", "OLD", "OLDqD", "OLDqR"], xall,
+           lambda e: e.tensor_copy(T.XB[:, 0:2432].indirect(T.DLU[:, 0:24]), T.OLD[:, 128:512]))
+        if send:
+            sb = "SB%d" % s
+            tt(["OW", "ND"], ["D2"], T.D2[:], T.OW[:, 32:40], T.ND[:], A.mult)
+            tt(["D2", "TL"], ["D3"], T.D3[:], T.D2[:], T.TL[:], A.add)
+            cp(["D3"], ["SLU"], T.SLU[:], T.D3[:])
+            op("v", ["SLU", "OLD"], [sb], lambda e: e.tensor_copy(T[sb][:, 0:256].indirect(T.SLU[:, 0:8]), T.OLD[:, 0:128]))
+            before("g", [sb], [])
+            g.remote_dma(T["ARR%d" % (s + 1)][:], T[sb][:, 0:32], T.sem["arr%d" % (s + 1)], T.sem.sent, pid, rid, wire)
+    dma("y", XR, ["y0"], T.y[:, 0:1024], T.XB[:, 256:1280])
+    dma("s", XR, ["y1"], T.y[:, 1024:2048], T.XB[:, 1280:2304])
+    g.wait_ge(T.sem.sent, nwire * (S - 1))
+    finish()

@@ -8,23 +8,24 @@ E11 = 2048.0
 OFFS = -8388608.0
 PEN = -33554432.0
 BASE = (96, 384, 1536)
-ORDER = "d0 s0 lc rq k3 x1 m0 d1 r2 s1 k1 m1 d2 s2 fe r3 fq k2 m2 d3 s3 m3 g6 x6 fa d4 s4 m4 m6 d5 s5 m5 p12 d7 s7 m7 fp fg pp lv r12 pg"
+SCAL = 4
+ORDER = "lc rq g3 k3 x1 d0 k1 r2 x3 fq fe d1 k2 ph d2 r3 s1 m1 d6 fa s2 d4 s6 d5 p12 m3 s0 s4 d7 m6 m2 m0 m4 fp lv fg pp s5 s7 m5 m7 r12 pg"
 
 SCRATCH = {}
 for _t, _l in (
         ("bfloat16", "XB:2432 QS:480 WTS:1 MT:128 MT2:128 ML:128 IO16:384 EK:2048 WR:2048 WBD:128 ONE:512 IB:128 NIB:128 IPEN:128"
-                     " IOFF:128 BDB:128 LTB:128 MKB:128 OCC1:512 OCC2:2048 OCC3:2048 AB1:512 AB2:2048 DF:8192 FE1:32 FQ2:128"
+                     " IOFF:128 BDB:128 LTB:128 MKB:64 OCC1:512 OCC2:2048 OCC3:2048 AB1:512 AB2:2048 DF:8192 FE1:32 DEAD:8 FQ2:128"
                      " FA:128 FB:128 FP:512 FG:512 OLD:512 ND:8 SB0:256 SB1:256 SB2:256 SB3:256 ARR1:32 ARR2:32 ARR3:32 ARR4:32"),
         ("float32", "KF:4 KG:4 KH:4 K32:4 MASK:384 PMF:1 LN0:8 LN:8 TRC:24 TRD:24 TL:8 IX3F:512 RS:32 RQ:2 RE:32 RF:2 LV:8 LIVE:8 NEQ:8"
-                    " M12:8 M3:8 MF:8 OWNF:24 CFM:8 GB:8 GO:8 W1:24 W2:24 W3:24 NE:8 D2:8 D3:8"),
-        ("float16", "IH:128 BDH:128 NTL:8 IX3:512 SELM:384"),
-        ("int32", "KKI:4 PIN:1 PMI:1 BH:8 PLW:2048 P1A:120 P1R:128 UI:128 U:128 Z:512 Y:512 MI:8 PG:8 PO:24"),
+                    " M12:8 M3:8 MD:8 ML12:8 CFM:8 CFX:8 CL:8 GO:8 W1:24 W2:24 W3:24 NE:8 D2:8 D3:8"),
+        ("float16", "IH:128 BDH:128 NTL:8 IX3:512 SELM:384 PH:160"),
+        ("int32", "KKI:4 PIN:1 PMI:1 BH:8 PLW:2048 P1A:120 UI:128 U:128 Z:512 Y:512 MI:8 PG:8 PO:24"),
         ("uint16", "OF:672 L1U:120 POU:24 XL:24 DLU:24 SLU:8")):
     for _w in _l.split():
         SCRATCH[_w.split(":")[0]] = ("sbuf", [128, int(_w.split(":")[1])], _t)
 for _n, _s, _t in (("QR", [128, 30, 1024], "bfloat16"), ("QRR", [128, 2, 512], "bfloat16"), ("IX12F", [128, 8, 20], "float32"),
                    ("IX12", [128, 8, 20], "float16"), ("NH", [128, 8, 4], "float32"), ("N1", [128, 8, 2], "float32"),
-                   ("OTHH", [128, 3, 128], "float16"), ("EQ", [128, 72, 128], "bfloat16")):
+                   ("OTHH", [128, 3, 128], "float16"), ("EQ", [128, 72, 128], "bfloat16"), ("JK", [128, 36, 112], "bfloat16")):
     SCRATCH[_n] = ("sbuf", _s, _t)
 BANKS = ("SD", "SR", "K12", "K3", "DA", "DB", "OT", "OW")
 for _n, _s in (("SD", [128, 128]), ("SR", [128, 128]), ("K12", [128, 8, 20]), ("K3", [128, 512]), ("DA", [128, 512]), ("DB", [128, 512]),
@@ -201,8 +202,6 @@ def rank_program(g, core, T, topo):
             mm([mat] + rd, bank, out, T[mat][:, 128 * r:128 * r + 128], rhs(r), start and r == 0, stop and r == 15)
 
     wrapsum("WR", ["QS"], "SD", T.SD[:, 0:30], lambda r: T.QS[:, r:480:16], True, True)
-    for r in range(16):
-        ts(["ML"], ["EK"], T.EK[:, 128 * r:128 * r + 128], T.ML[:], float(r), E11, A.is_equal, A.mult)
     places(["SD"], T.SD[:, 0:30], 30, T.P1A[:], "P1A")
     cp(["P1A"], ["L1U"], T.L1U[:], T.P1A[:])
     w = 16
@@ -210,22 +209,25 @@ def rank_program(g, core, T, topo):
         act(["QR0"], ["QR0"], T.QR[:, 0:6, w:2 * w], T.QR[:, 0:6, 0:w], ACT.Copy)
         w *= 2
     dma("y", ["QR0"], ["QX0"], T.QR[:, 0:6, 512:1024], T.QR[:, 0:6, 0:512])
-    ts(["IB"], ["NIB"], T.NIB[:], T.IB[:], -1.0, None, A.mult)
-    ts(["IB"], ["IPEN"], T.IPEN[:], T.IB[:], PEN, None, A.mult)
-    ts(["IB"], ["IOFF"], T.IOFF[:], T.IB[:], OFFS, None, A.mult)
-    cp(["IX12F"], ["IX12"], T.IX12[:], T.IX12F[:])
-    cp(["IX3F"], ["IX3"], T.IX3[:], T.IX3F[:])
-    cp(["IB"], ["IH"], T.IH[:], T.IB[:])
-    ts(["ML"], ["BDB"], T.BDB[:], T.ML[:], 0.0, None, A.is_ge)
-    ts(["ML"], ["BDH"], T.BDH[:], T.ML[:], 0.0, None, A.is_ge)
-    ts(["ML", "WTS"], ["WBD"], T.WBD[:], T.ML[:], 0.0, T.WTS[:, 0:1], A.is_ge, A.mult)
-    ts(["PIN"], ["PMI"], T.PMI[:], T.PIN[:], 15, None, A.bitwise_and)
-    cp(["PMI"], ["PMF"], T.PMF[:], T.PMI[:])
-    ts(["LN0", "PMF"], ["LN"], T.LN[:], T.LN0[:], T.PMF[:, 0:1], None, A.add)
-    ts(["LN", "PLW0"], ["PLWA"], T.PLW[:, 24:32], T.LN[:], -256.0, None, A.add)
-    ts(["LN", "PLW0"], ["PLWB"], T.PLW[:, 8:16], T.LN[:], -128.0, None, A.add)
-    sel("BDB", "LTB", T.LTB[:], T.BDB[:], [[1, 128]], A.is_gt, 0.0, 0, -1)
     XR = ["XBx", "XBx2"]
+
+    def constants():
+        for r in range(16):
+            ts(["ML"], ["EK"], T.EK[:, 128 * r:128 * r + 128], T.ML[:], float(r), E11, A.is_equal, A.mult)
+        ts(["IB"], ["NIB"], T.NIB[:], T.IB[:], -1.0, None, A.mult)
+        ts(["IB"], ["IPEN"], T.IPEN[:], T.IB[:], PEN, None, A.mult)
+        ts(["IB"], ["IOFF"], T.IOFF[:], T.IB[:], OFFS, None, A.mult)
+        cp(["IX12F"], ["IX12"], T.IX12[:], T.IX12F[:])
+        cp(["IX3F"], ["IX3"], T.IX3[:], T.IX3F[:])
+        cp(["IB"], ["IH"], T.IH[:], T.IB[:])
+        ts(["ML"], ["BDB"], T.BDB[:], T.ML[:], 0.0, None, A.is_ge)
+        ts(["ML"], ["BDH"], T.BDH[:], T.ML[:], 0.0, None, A.is_ge)
+        ts(["ML", "WTS"], ["WBD"], T.WBD[:], T.ML[:], 0.0, T.WTS[:, 0:1], A.is_ge, A.mult)
+        ts(["PIN"], ["PMI"], T.PMI[:], T.PIN[:], 15, None, A.bitwise_and)
+        cp(["PMI"], ["PMF"], T.PMF[:], T.PMI[:])
+        ts(["LN0", "PMF"], ["LN"], T.LN[:], T.LN0[:], T.PMF[:, 0:1], None, A.add)
+        ts(["LN", "PLW0"], ["PLWA"], T.PLW[:, 24:32], T.LN[:], -256.0, None, A.add)
+        ts(["LN", "PLW0"], ["PLWB"], T.PLW[:, 8:16], T.LN[:], -128.0, None, A.add)
 
     def gather(q, rd, wr, out, lst):
         if q == "v":
@@ -243,8 +245,14 @@ def rank_program(g, core, T, topo):
         mm(["NIB", rt], bank, ps, T.NIB[:], reps, False, True)
         act([bank], [otok], out, ps, ACT.Abs)
 
+    def first(s):
+        gather("s", ["L1U"], ["OCC1Ds"], T.OCC1[:, 0:192], T.L1U[:, 24 * s:24 * s + 12])
+        gather("v", ["L1U"], ["OCC1Dv"], T.OCC1[:, 192:384], T.L1U[:, 24 * s + 12:24 * s + 24])
+        cp(["P1A"], ["PLW1D"], T.PLW[:, 96:120], T.P1A[:, 24 * s:24 * s + 24])
+
     for s in range(S):
         arrivals = s > 0
+        send = s + 1 < S
         H = 8 if arrivals else 6
         both = ("D", "R") if arrivals else ("D",)
         at, qt = "ARR%d" % s, "QR%d" % s
@@ -254,11 +262,12 @@ def rank_program(g, core, T, topo):
             outside("arr%d" % s, nland, [at])
             dma("y", [], ["XBqD"], T.XB[:, 0:96], T.qs[:, 96 * s:96 * s + 96])
             dma("y", [], ["OLDqD"], T.OLD[:, 384:480], T.qs[:, 96 * s:96 * s + 96])
+        else:
+            first(0)
+            constants()
 
-        gather("s", ["L1U"], ["OCC1D"], T.OCC1[:, 0:384], T.L1U[:, 24 * s:24 * s + 24])
-        cp(["P1A"], ["PLW1D"], T.PLW[:, 96:120], T.P1A[:, 24 * s:24 * s + 24])
-        wrapsum("WR", ["OCC1D"], "SD", T.SD[:, 0:24], lambda r: T.OCC1[:, r:384:16], True, True)
-        diff(["OCC1D"], qt, T.OCC1[:, 0:384], T.QR[:, 6 * s:6 * s + 6, 0:64], 384, T.AB1[:, 0:384], "AB1D")
+        wrapsum("WR", ["OCC1Ds", "OCC1Dv"], "SD", T.SD[:, 0:24], lambda r: T.OCC1[:, r:384:16], True, True)
+        diff(["OCC1Ds", "OCC1Dv"], qt, T.OCC1[:, 0:384], T.QR[:, 6 * s:6 * s + 6, 0:64], 384, T.AB1[:, 0:384], "AB1D")
         places(["SD"], T.SD[:, 0:24], 24, T.PLW[:, 384:480], "PLW2D")
         cp(["PLW2D"], ["OF2D"], T.OF[:, 32:128], T.PLW[:, 384:480])
         gather("s", ["OF2D"], ["OCC2Ds"], T.OCC2[:, 0:768], T.OF[:, 32:80])
@@ -279,7 +288,7 @@ def rank_program(g, core, T, topo):
                 w *= 2
             dma("y", [at], ["XBqR"], T.XB[:, 96:128], arr[:])
             dma("y", [at], ["OLDqR"], T.OLD[:, 480:512], arr[:])
-        if s + 1 < S:
+        if send:
             w, nt, lo = 16, "QR%d" % (s + 1), 6 * (s + 1)
             while w < 512:
                 sel(nt, nt, T.QR[:, lo:lo + 6, w:2 * w], T.QR[:, lo:lo + 6, 0:w], [[0, 6], [0, w]], A.is_equal, 0.0, 0, 0)
@@ -306,17 +315,17 @@ def rank_program(g, core, T, topo):
             wrapsum("EK", ["DF%d" % hi], "K3", T.K3[:, 64 * hi:64 * hi + 64], lambda r: T.DF[:, 1024 * hi + r:1024 * hi + 1024:16], False, False)
 
         def p_g(hi):
-            k = hi - 6
-            gather("s", ["OF3R"], ["OCC3%d" % k], T.OCC3[:, 1024 * k:1024 * k + 1024], T.OF[:, 544 + 64 * k:608 + 64 * k])
+            k = 1024 * (hi % 2)
+            gather("s", ["OF3D" if hi < 6 else "OF3R"], ["OCC3%d" % (hi % 2)], T.OCC3[:, k:k + 1024], T.OF[:, 160 + 64 * hi:224 + 64 * hi])
 
         def p_x(hi):
             if hi == 1:
                 diff(["OCC1R"], "QRR", T.OCC1[:, 384:512], T.QRR[:, :, 0:64], 128, T.AB1[:, 384:512], "AB1R")
                 return
-            k = hi - 6
             for c in range(2):
-                o = 1024 * k + 512 * c
-                diff(["OCC3%d" % k], "QRR", T.OCC3[:, o:o + 512], T.QRR[:, k, :], 512, T.DF[:, 6144 + o:6144 + o + 512], "DF%d" % hi)
+                o, k = 1024 * hi + 512 * c, 1024 * (hi % 2) + 512 * c
+                reps = T.QR[:, 6 * s + hi, 0:512] if hi < 6 else T.QRR[:, hi - 6, :]
+                diff(["OCC3%d" % (hi % 2)], qt if hi < 6 else "QRR", T.OCC3[:, k:k + 512], reps, 512, T.DF[:, o:o + 512], "DF%d" % hi)
 
         def p_rq():
             mm(["WBD", at], "SR", T.SR[:, 0:32], T.WBD[:], arr[:], True, True)
@@ -350,11 +359,12 @@ def rank_program(g, core, T, topo):
                 ts(["LN"], ["TRD"], T.TRD[:, 8 * t:8 * t + 8], T.LN[:], -1.0, 256.0 - c, A.mult, A.add)
             ts(["LN"], ["TL"], T.TL[:], T.LN[:], 128.0, None, A.add)
             ts(["TL"], ["NTL"], T.NTL[:], T.TL[:], -1.0, None, A.mult)
-            vset("MKB", T.MKB[:, 0:112], 0.0)
-            ts(["IO16", "PMF"], ["MKB"], T.MKB[:, 112:128], T.IO16[:, 0:16], T.PMF[:, 0:1], -16.0, A.is_ge, A.mult)
+            vset("CL0", T.CL[:], 0.0)
+            ts(["IO16", "PMF"], ["MKB"], T.MKB[:], T.IO16[:, 0:64], T.PMF[:, 0:1], -16.0, A.is_ge, A.mult)
             for i in range(S - 1):
                 vset("SB%d" % i, T["SB%d" % i][:], 512.0)
             vset("OLDqR", T.OLD[:, 480:512], 0.0)
+            sel("BDB", "LTB", T.LTB[:], T.BDB[:], [[1, 128]], A.is_gt, 0.0, 0, -1)
 
         def p_k3():
             mm(["IOFF", "ONE"], "K3", T.K3[:, 0:64 * H], T.IOFF[:], T.ONE[:, 0:64 * H], True, False)
@@ -390,15 +400,20 @@ def rank_program(g, core, T, topo):
                 for f in ("FA", "FB"):
                     mm(["IPEN", f], "K3", T.K3[:, a:64 * H:4], T.IPEN[:], T[f][:, 0:16 * H], False, False)
 
+        def p_ph():
+            cp(PL1, ["PH1"], T.PH[:, 0:4 * H], T.PLW[:, 96:96 + 4 * H])
+            cp(PL2, ["PH2"], T.PH[:, 32:32 + 16 * H], T.PLW[:, 384:384 + 16 * H])
+            mm(["IH", "PH2"], "OT", T.OT[:, 0:16 * H], T.IH[:], T.PH[:, 32:32 + 16 * H], True, True)
+            for a in range(4):
+                mm(["IH", "PH1"], "OT", T.OT[:, 128 + a:128 + 16 * H:4], T.IH[:], T.PH[:, 0:4 * H], True, True)
+
         def p_fp():
             for a in range(4):
-                tt(PL3 + PL2, ["FP"], T.FP[:, a:64 * H:4], T.PLW[:, 1536 + a:1536 + 64 * H:4], T.PLW[:, 384:384 + 16 * H], A.is_equal)
+                tt(PL3 + ["OT"], ["FP"], T.FP[:, a:64 * H:4], T.PLW[:, 1536 + a:1536 + 64 * H:4], T.OT[:, 0:16 * H], A.is_equal)
 
         def p_fg():
             for a in range(4):
-                cp(PL1, ["P1R"], T.P1R[:, a:16 * H:4], T.PLW[:, 96:96 + 4 * H])
-            for a in range(4):
-                tt(PL3 + ["P1R"], ["FG"], T.FG[:, a:64 * H:4], T.PLW[:, 1536 + a:1536 + 64 * H:4], T.P1R[:, 0:16 * H], A.is_equal)
+                tt(PL3 + ["OT"], ["FG"], T.FG[:, a:64 * H:4], T.PLW[:, 1536 + a:1536 + 64 * H:4], T.OT[:, 128:128 + 16 * H], A.is_equal)
 
         def p_pp():
             mm(["IPEN", "FP"], "K3", T.K3[:, 0:64 * H], T.IPEN[:], T.FP[:, 0:64 * H], False, False)
@@ -410,16 +425,21 @@ def rank_program(g, core, T, topo):
             tt(["NH"], ["N1"], T.N1[:], T.NH[:, :, 0:2], T.NH[:, :, 2:4], A.mult)
             tt(["N1"], ["LV"], T.LV[:], T.N1[:, :, 0], T.N1[:, :, 1], A.mult)
             tt(["LV", "NEQ"], ["LIVE"], T.LIVE[:], T.LV[:], T.NEQ[:], A.mult)
+            ts(["LIVE"], ["MD"], T.MD[:], T.LIVE[:], -33554432.0, 16777216.0, A.mult, A.add)
+            ts(["LIVE"], ["DEAD"], T.DEAD[:], T.LIVE[:], -16.0, 16.0, A.mult, A.add)
 
         def p_r12():
             for hi in range(H):
                 red(["K12"], ["M12"], T.M12[:, hi:hi + 1], T.K12[:, hi, :], A.max)
+            tt(["M12", "MD"], ["ML12"], T.ML12[:], T.M12[:], T.MD[:], A.max)
 
         by_block = {"d": p_d, "s": p_s, "m": p_m, "g": p_g, "x": p_x}
         whole = {"rq": p_rq, "r2": p_r2, "r3": p_r3, "lc": p_lc, "k3": p_k3, "k1": p_k1, "fe": p_fe, "fq": p_fq, "k2": p_k2, "fa": p_fa,
-                 "p12": p_p12, "fp": p_fp, "fg": p_fg, "pp": p_pp, "pg": p_pg, "lv": p_lv, "r12": p_r12}
+                 "p12": p_p12, "fp": p_fp, "fg": p_fg, "pp": p_pp, "ph": p_ph, "pg": p_pg, "lv": p_lv, "r12": p_r12}
         for w in ORDER.split():
-            if w == "lc" and s > 0 or not arrivals and (w[0] == "r" and w != "r12" or w in ("x1", "d6", "s6", "m6", "g6", "x6", "d7", "s7", "m7", "g7", "x7")):
+            if w == "lc" and s > 0:
+                continue
+            if not arrivals and (w in ("rq", "r2", "r3", "x1") or w[0] in "dsmgx" and w[1:] in ("6", "7")):
                 continue
             if w in whole:
                 whole[w]()
@@ -428,43 +448,52 @@ def rank_program(g, core, T, topo):
 
         for hi in range(H):
             red(["K3"], ["M3"], T.M3[:, hi:hi + 1], T.K3[:, 64 * hi:64 * hi + 64], A.max)
-        tt(["M12", "M3"], ["MF"], T.MF[:], T.M12[:], T.M3[:], A.max)
-        tt(["MF", "LIVE"], ["MI"], T.MI[:], T.MF[:], T.LIVE[:], A.mult)
+        tt(["ML12", "M3"], ["MI"], T.MI[:], T.ML12[:], T.M3[:], A.max)
         ts(["MI"], ["PG"], T.PG[:], T.MI[:], 4, 127, A.arith_shift_right, A.bitwise_and)
         ts(["MI"], ["PO"], T.PO[:, 0:8], T.MI[:], 2047, None, A.bitwise_and)
         ts(["MI"], ["PO"], T.PO[:, 8:16], T.MI[:], 2, 511, A.arith_shift_right, A.bitwise_and)
         tt(["PG", "BH"], ["PO"], T.PO[:, 16:24], T.PG[:], T.BH[:], A.max)
         cp(["PO"], ["POU"], T.POU[:], T.PO[:])
-        ts(["MF"], ["NE"], T.NE[:], T.MF[:], 0.0, None, A.is_lt)
+        ts(["MI"], ["NE"], T.NE[:], T.MI[:], 0.0, None, A.is_lt)
         tt(["POU", "MASK", "PLW0", "PLWA", "PLWB"] + PL1 + PL2 + PL3, ["SELM"],
            T.SELM[:], T.PLW[:, 0:2048].indirect(T.POU[:, 0:24]), T.MASK[:], A.mult)
         mm(["BDH", "SELM"], "OT", T.OT[:], T.BDH[:], T.SELM[:], True, True)
         for r in range(16):
             mm(["IH", "SELM"], "OW", T.OW[:, 0:24], T.IH[:], T.SELM[:, r:384:16], r == 0, r == 15)
         cp(["OT"], ["OTHH"], T.OTHH[:], T.OT[:])
-        act(["OW"], ["OWNF"], T.OWNF[:], T.OW[:, 0:24], ACT.Copy)
-        ts(["OWNF"], ["XL"], T.XL[:], T.OWNF[:], 256.0, None, A.add)
+        ts(["OW"], ["XL"], T.XL[:], T.OW[:, 0:24], 256.0, None, A.add)
         xall = XR + ["XBqD", "XBqR", "XBq", "XBt", "XBt2"]
-        act(["XL"] + xall, ["OLD"], T.OLD[:, 0:384], T.XB[:, 0:2432].indirect(T.XL[:, 0:24]), ACT.Copy)
+
+        def own_blocks(h0):
+            out = T.DB[:, 16 * h0:16 * h0 + 64]
+            mm(["IB", "MKB"], "DB", out, T.IB[:], T.MKB[:], True, False)
+            mm(["IB", "DEAD"], "DB", T.DB[:, 16 * h0:16 * h0 + 64:16], T.IB[:], T.DEAD[:, h0:h0 + 4], False, False)
+            for k in range(9):
+                mm(["IB"] + ["EQ%d" % h for h in range(h0, h0 + 4)], "DB", out, T.IB[:],
+                   T.EQ[:, 8 * k + h0:8 * k + h0 + 4, 112:128], False, k == 8)
+
         for hi in range(7, -1, -1):
             n = 16 * (hi + 1)
-            bank, o = ("DA", 8 * hi * (hi + 1)) if hi < 6 else ("DB", 112 * (hi - 6))
-            out = T[bank][:, o:o + n]
-            mm(["IB", "MKB"], bank, out, T.IB[:], T.MKB[:, 128 - n:128], True, False)
             for t in range(3):
-                k = 3 * (3 * hi + t)
-                ts(["OTHH", "OWNF"], ["EQ%d" % k], T.EQ[:, k:k + 3, 0:n], T.OTHH[:, :, 0:n],
-                   T.OWNF[:, 8 * t + hi:8 * t + hi + 1], None, A.is_equal)
-                for t2 in range(3):
-                    mm(["IB", "EQ%d" % k], bank, out, T.IB[:], T.EQ[:, k + t2, 0:n], False, t == 2 and t2 == 2)
-        tt(["OWNF", "TRD"], ["W1"], T.W1[:], T.OWNF[:], T.TRD[:], A.add)
+                ts(["OTHH", "OW"], ["EQ%d" % hi], T.EQ[:, 24 * t + hi:24 * t + hi + 17:8, 128 - n:128], T.OTHH[:, :, 0:n],
+                   T.OW[:, 8 * t + hi:8 * t + hi + 1], None, A.is_equal)
+            if hi >= SCAL:
+                k = 9 * (hi - SCAL)
+                op("s", ["EQ%d" % hi], ["CL%d" % hi, "JK%d" % hi], lambda e: e.activation(
+                    T.JK[:, k:k + 9, 0:16 * hi], T.EQ[:, hi:72:8, 112 - 16 * hi:112], ACT.Copy, accum_out=T.CL[:, hi:hi + 1]))
+            elif hi > 0:
+                for k in range(9):
+                    mm(["IB", "EQ%d" % hi], "DA", T.DA[:, 64 * hi:80 * hi], T.IB[:], T.EQ[:, 8 * k + hi, 112 - 16 * hi:112], k == 0, k == 8)
+            if hi in (4, 0):
+                own_blocks(hi)
+        act(["XL"] + xall, ["OLD"], T.OLD[:, 0:384], T.XB[:, 0:2432].indirect(T.XL[:, 0:24]), ACT.Copy)
+        tt(["OW", "TRD"], ["W1"], T.W1[:], T.OW[:, 0:24], T.TRD[:], A.add)
+        for hi in range(SCAL - 1, 0, -1):
+            red(["DA"], ["CL%d" % hi], T.CL[:, hi:hi + 1], T.DA[:, 64 * hi:80 * hi], A.max)
         for hi in range(7, -1, -1):
-            n = 16 * (hi + 1)
-            bank, o = ("DA", 8 * hi * (hi + 1)) if hi < 6 else ("DB", 112 * (hi - 6))
-            red([bank], ["CFM"], T.CFM[:, hi:hi + 1], T[bank][:, o:o + n], A.max)
-        ts(["CFM"], ["GB"], T.GB[:], T.CFM[:], 0.5, None, A.is_lt)
-        tt(["GB", "LIVE"], ["GO"], T.GO[:], T.GB[:], T.LIVE[:], A.mult)
-        send = s + 1 < S
+            red(["DB"], ["CFM"], T.CFM[:, hi:hi + 1], T.DB[:, 16 * hi:16 * hi + 16], A.max)
+        tt(["CFM", "CL0"] + ["CL%d" % h for h in range(1, 8)], ["CFX"], T.CFX[:], T.CFM[:], T.CL[:], A.max)
+        ts(["CFX"], ["GO"], T.GO[:], T.CFX[:], 0.5, None, A.is_lt)
         if send:
             tt(["GO", "NE"], ["ND"], T.ND[:], T.GO[:], T.NE[:], A.mult)
             mm(["IH", "NTL"], "OW", T.OW[:, 32:40], T.IH[:], T.NTL[:], True, False)
@@ -478,6 +507,7 @@ def rank_program(g, core, T, topo):
         op("v", ["DLU", "OLD", "OLDqD", "OLDqR"], xall,
            lambda e: e.tensor_copy(T.XB[:, 0:2432].indirect(T.DLU[:, 0:24]), T.OLD[:, 128:512]))
         if send:
+            first(s + 1)
             sb = "SB%d" % s
             tt(["OW", "ND"], ["D2"], T.D2[:], T.OW[:, 32:40], T.ND[:], A.mult)
             tt(["D2", "TL"], ["D3"], T.D3[:], T.D2[:], T.TL[:], A.add)

from concourse.mybir import AluOpType, AxisListType, ActivationFunctionType

A = AluOpType
ACT = ActivationFunctionType
X = AxisListType.X
S = 5
E11 = 2048.0
OFFS = -8388608.0
PEN = -33554432.0
BASE = (96, 384, 1536)
SCAL = 4
ORDER = "lc rq g3 k3 x1 d0 k1 r2 x3 fq fe d1 k2 ph d2 r3 s1 m1 d6 fa s2 d4 s6 d5 p12 m3 s0 s4 d7 m6 m2 m0 m4 fp lv fg pp s5 s7 m5 m7 r12 pg"

SCRATCH = {}
for _t, _l in (
        ("bfloat16", "XB:2432 QS:480 WTS:1 MT:128 MT2:128 ML:128 IO16:384 EK:2048 WR:2048 WBD:128 ONE:512 IB:128 NIB:128 IPEN:128"
                     " IOFF:128 BDB:128 LTB:128 MKB:64 OCC1:512 OCC2:2048 OCC3:2048 AB1:512 AB2:2048 DF:8192 FE1:32 DEAD:8 FQ2:128"
                     " FA:128 FB:128 FP:512 FG:512 OLD:512 ND:8 SB0:256 SB1:256 SB2:256 SB3:256 ARR1:32 ARR2:32 ARR3:32 ARR4:32"),
        ("float32", "KF:4 KG:4 KH:4 K32:4 MASK:384 PMF:1 LN0:8 LN:8 TRC:24 TRD:24 TL:8 IX3F:512 RS:32 RQ:2 RE:32 RF:2 LV:8 LIVE:8 NEQ:8"
                    " M12:8 M3:8 MD:8 ML12:8 CFM:8 CFX:8 CL:8 GO:8 W1:24 W2:24 W3:24 NE:8 D2:8 D3:8"),
        ("float16", "IH:128 BDH:128 NTL:8 IX3:512 SELM:384 PH:160"),
        ("int32", "KKI:4 PIN:1 PMI:1 BH:8 PLW:2048 P1A:120 UI:128 U:128 Z:512 Y:512 MI:8 PG:8 PO:24"),
        ("uint16", "OF:672 L1U:120 POU:24 XL:24 DLU:24 SLU:8")):
    for _w in _l.split():
        SCRATCH[_w.split(":")[0]] = ("sbuf", [128, int(_w.split(":")[1])], _t)
for _n, _s, _t in (("QR", [128, 30, 1024], "bfloat16"), ("QRR", [128, 2, 512], "bfloat16"), ("IX12F", [128, 8, 20], "float32"),
                   ("IX12", [128, 8, 20], "float16"), ("NH", [128, 8, 4], "float32"), ("N1", [128, 8, 2], "float32"),
                   ("OTHH", [128, 3, 128], "float16"), ("EQ", [128, 72, 128], "bfloat16"), ("JK", [128, 36, 112], "bfloat16")):
    SCRATCH[_n] = ("sbuf", _s, _t)
BANKS = ("SD", "SR", "K12", "K3", "DA", "DB", "OT", "OW")
for _n, _s in (("SD", [128, 128]), ("SR", [128, 128]), ("K12", [128, 8, 20]), ("K3", [128, 512]), ("DA", [128, 512]), ("DB", [128, 512]),
               ("OT", [128, 384]), ("OW", [128, 64])):
    SCRATCH[_n] = ("psum", _s, "float32")
SEMAPHORES = ["cv", "cs", "cp", "cg", "sent"] + ["arr%d" % (i + 1) for i in range(S - 1)] + ["d%d" % i for i in range(40)]


def make_queue(g, T):
    eng = {"v": g.vector, "s": g.scalar, "p": g.tensor, "g": g, "y": g.sync}
    count = {"cv": 0, "cs": 0, "cp": 0, "cg": 0}
    known = {q: {} for q in eng}
    snap, writer, readers, touch = {}, {}, {}, {}
    dmas = [0]

    def before(q, rd, wr):
        evs = []
        for t in rd:
            if t in BANKS:
                evs += [e for e in touch.get(t, {}).values() if e[2] != q]
            elif t in writer:
                evs.append(writer[t])
        for t in wr:
            if t in BANKS:
                evs += [e for e in touch.get(t, {}).values() if e[2] != q]
            elif readers.get(t):
                evs += list(readers[t].values()) + ([writer[t]] if t in writer else [])
            elif t in writer and writer[t][2] != q:
                evs.append(writer[t])
        best = {}
        for sem, val, _ in evs:
            best[sem] = max(best.get(sem, 0), val)
        for sem in sorted(best):
            val = best[sem]
            if known[q].get(sem, 0) < val:
                eng[q].wait_ge(T.sem[sem], val)
                for k, n in snap.get((sem, val), {}).items():
                    known[q][k] = max(known[q].get(k, 0), n)
                known[q][sem] = val

    def after(ev, rd, wr):
        for t in rd:
            if t in BANKS:
                touch.setdefault(t, {})[ev[2]] = ev
            else:
                readers.setdefault(t, {})[(ev[2], ev[0])] = ev
        for t in wr:
            if t in BANKS:
                touch.setdefault(t, {})[ev[2]] = ev
            else:
                writer[t] = ev
                readers[t] = {}

    def op(q, rd, wr, call):
        before(q, rd, wr)
        sem = "c" + q
        count[sem] += 1
        call(eng[q]).then_inc(T.sem[sem], 1)
        snap[(sem, count[sem])] = dict(known[q])
        after((sem, count[sem], q), rd, wr)

    def dma(q, rd, wr, out, in_):
        before(q, rd, wr)
        sem = "d%d" % dmas[0]
        dmas[0] += 1
        eng[q].dma_start(out, in_).then_inc(T.sem[sem], 16)
        snap[(sem, 16)] = dict(known[q])
        after((sem, 16, "dma"), rd, wr)

    def outside(sem, val, wr):
        after((sem, val, "far"), [], wr)

    def finish():
        for sem in ("cv", "cs", "cp", "cg"):
            if known["g"].get(sem, 0) < count[sem]:
                g.wait_ge(T.sem[sem], count[sem])
        for i in range(dmas[0]):
            g.wait_ge(T.sem["d%d" % i], 16)
    return op, dma, outside, before, finish


def rank_program(g, core, T, topo):
    rank = T.rank_of(core)
    if rank is None:
        return
    op, dma, outside, before, finish = make_queue(g, T)
    nxt = T.cores[(rank + 1) % len(T.cores)]
    rid, pid = topo.addr(nxt, core)
    wire = topo.mask(core, nxt)
    nwire = len(topo.engines(core, nxt))
    nland = len(topo.engines(T.cores[(rank - 1) % len(T.cores)], core))

    dma("y", [], ["QS"], T.QS[:], T.qs[:])
    dma("s", [], ["WTS"], T.WTS[:], T.wt[:])
    dma("s", [], ["KKI"], T.KKI[:], T.kk[:])
    dma("y", [], ["QR0"], T.QR[:, 0:6, 0:16], T.qs[:, 0:96])
    dma("s", [], ["XBx"], T.XB[:, 256:1280], T.x0[:, 0:1024])
    dma("y", [], ["XBx2"], T.XB[:, 1280:2304], T.x0[:, 1024:2048])
    for s in range(1, S):
        dma("y", [], ["QR%d" % s], T.QR[:, 6 * s:6 * s + 6, 0:16], T.qs[:, 96 * s:96 * s + 96])
    dma("y", [], ["XBqD"], T.XB[:, 0:96], T.qs[:, 0:96])
    dma("y", [], ["OLDqD"], T.OLD[:, 384:480], T.qs[:, 0:96])

    def iota(tok, out, pattern, base, cm, small=True):
        if small:
            op("g", [], [tok], lambda e: e.iota(out, pattern, base, cm, allow_small_or_imprecise_dtypes=True))
        else:
            op("g", [], [tok], lambda e: e.iota(out, pattern, base, cm))

    def sel(rd, tok, out, in_, pattern, cmp, fill, base, cm):
        op("g", [rd], [tok], lambda e: e.affine_select(out, in_, pattern, cmp, fill, base, cm))

    def vset(tok, out, c):
        op("v", [], [tok], lambda e: e.memset(out, c))

    def ts(rd, wr, out, in0, s1, s2, op0, op1=None):
        if op1 is None:
            op("v", rd, wr, lambda e: e.tensor_scalar(out, in0, s1, None, op0=op0))
        else:
            op("v", rd, wr, lambda e: e.tensor_scalar(out, in0, s1, s2, op0=op0, op1=op1))

    def tt(rd, wr, out, a, b, o):
        op("v", rd, wr, lambda e: e.tensor_tensor(out, a, b, o))

    def cp(rd, wr, out, a):
        op("v", rd, wr, lambda e: e.tensor_copy(out, a))

    def red(rd, wr, out, a, o):
        op("v", rd, wr, lambda e: e.tensor_reduce(out, a, X, o))

    def act(rd, wr, out, a, func):
        op("s", rd, wr, lambda e: e.activation(out, a, func))

    def mm(rd, bank, out, lhsT, rhs, start, stop):
        op("p", rd, [bank], lambda e: e.matmul(out, lhsT, rhs, start, stop))

    iota("MT", T.MT[:], [[0, 8], [1, 16]], 0, 0)
    sel("MT", "MT2", T.MT2[:], T.MT[:], [[-16, 8], [0, 16]], A.is_ge, -1.0, 0, 1)
    sel("MT2", "ML", T.ML[:], T.MT2[:], [[16, 8], [0, 16]], A.is_ge, -1.0, 15, -1)
    vset("ONE", T.ONE[:], 1.0)
    sel("ONE", "IB", T.IB[:], T.ONE[:, 0:128], [[-1, 128]], A.is_equal, 0.0, 0, 1)
    iota("PIN", T.PIN[:], [[0, 1]], 0, 1, False)
    iota("IO16", T.IO16[:], [[0, 24], [1, 16]], 0, 0)
    iota("LN0", T.LN0[:], [[16, 8]], 0, 0)
    iota("BH", T.BH[:], [[1, 8]], 8, 0, False)
    iota("IX12F", T.IX12F[:, :, 0:4], [[4, 8], [1, 4]], BASE[0], 0)
    iota("IX12F", T.IX12F[:, :, 4:20], [[16, 8], [1, 16]], BASE[1], 0)
    iota("IX3F", T.IX3F[:], [[1, 512]], BASE[2], 0)
    op("v", [], ["XBq", "XBt"], lambda e: e.memset(T.XB[:, 96:256], 0.0))
    vset("XBt2", T.XB[:, 2304:2432], 0.0)
    vset("PLW0", T.PLW[:], -256)
    vset("NH", T.NH[:], 0.0)
    vset("M12", T.M12[:], OFFS)
    vset("M3", T.M3[:], OFFS)
    vset("NEQ", T.NEQ[:], 1.0)
    for r in range(16):
        ts(["ML", "WTS"], ["WR"], T.WR[:, 128 * r:128 * r + 128], T.ML[:], float(r), T.WTS[:, 0:1], A.is_equal, A.mult)
    cp(["KKI"], ["KF"], T.KF[:], T.KKI[:])
    ts(["KF"], ["KG"], T.KG[:], T.KF[:], 1024.0, -2048.0, A.is_gt, A.mult)
    tt(["KF", "KG"], ["KH"], T.KH[:], T.KF[:], T.KG[:], A.add)
    ts(["KH"], ["K32"], T.K32[:], T.KH[:], 32.0, None, A.mult)

    def places(rd, src, n, dst, dtok):
        cp(rd, ["UI"], T.UI[:, 0:n], src)
        ts(["UI"], ["U"], T.U[:, 0:n], T.UI[:, 0:n], 2047, None, A.bitwise_and)
        for a in range(4):
            ts(["U", "K32"], ["Z%d" % a], T.Z[:, a * n:a * n + n], T.U[:, 0:n], T.K32[:, a:a + 1], None, A.add)
        for a in range(4):
            tt(["Z%d" % a, "U"], ["Y"], T.Y[:, a:4 * n:4], T.Z[:, a * n:a * n + n], T.U[:, 0:n], A.mult)
        ts(["Y"], [dtok], dst, T.Y[:, 0:4 * n], 5, 2047, A.arith_shift_right, A.bitwise_and)

    def wrapsum(mat, rd, bank, out, rhs, start, stop):
        for r in range(16):
            mm([mat] + rd, bank, out, T[mat][:, 128 * r:128 * r + 128], rhs(r), start and r == 0, stop and r == 15)

    wrapsum("WR", ["QS"], "SD", T.SD[:, 0:30], lambda r: T.QS[:, r:480:16], True, True)
    places(["SD"], T.SD[:, 0:30], 30, T.P1A[:], "P1A")
    cp(["P1A"], ["L1U"], T.L1U[:], T.P1A[:])
    w = 16
    while w < 512:
        act(["QR0"], ["QR0"], T.QR[:, 0:6, w:2 * w], T.QR[:, 0:6, 0:w], ACT.Copy)
        w *= 2
    dma("y", ["QR0"], ["QX0"], T.QR[:, 0:6, 512:1024], T.QR[:, 0:6, 0:512])
    XR = ["XBx", "XBx2"]

    def constants():
        for r in range(16):
            ts(["ML"], ["EK"], T.EK[:, 128 * r:128 * r + 128], T.ML[:], float(r), E11, A.is_equal, A.mult)
        ts(["IB"], ["NIB"], T.NIB[:], T.IB[:], -1.0, None, A.mult)
        ts(["IB"], ["IPEN"], T.IPEN[:], T.IB[:], PEN, None, A.mult)
        ts(["IB"], ["IOFF"], T.IOFF[:], T.IB[:], OFFS, None, A.mult)
        cp(["IX12F"], ["IX12"], T.IX12[:], T.IX12F[:])
        cp(["IX3F"], ["IX3"], T.IX3[:], T.IX3F[:])
        cp(["IB"], ["IH"], T.IH[:], T.IB[:])
        ts(["ML"], ["BDB"], T.BDB[:], T.ML[:], 0.0, None, A.is_ge)
        ts(["ML"], ["BDH"], T.BDH[:], T.ML[:], 0.0, None, A.is_ge)
        ts(["ML", "WTS"], ["WBD"], T.WBD[:], T.ML[:], 0.0, T.WTS[:, 0:1], A.is_ge, A.mult)
        ts(["PIN"], ["PMI"], T.PMI[:], T.PIN[:], 15, None, A.bitwise_and)
        cp(["PMI"], ["PMF"], T.PMF[:], T.PMI[:])
        ts(["LN0", "PMF"], ["LN"], T.LN[:], T.LN0[:], T.PMF[:, 0:1], None, A.add)
        ts(["LN", "PLW0"], ["PLWA"], T.PLW[:, 24:32], T.LN[:], -256.0, None, A.add)
        ts(["LN", "PLW0"], ["PLWB"], T.PLW[:, 8:16], T.LN[:], -128.0, None, A.add)

    def gather(q, rd, wr, out, lst):
        if q == "v":
            cp(rd + XR, wr, out, T.XB[:, 256:2304].indirect(lst))
        else:
            act(rd + XR, wr, out, T.XB[:, 256:2304].indirect(lst), ACT.Copy)

    diffs = [0]

    def diff(rd, rt, occ, reps, n, out, otok):
        bank = ("DA", "DB")[diffs[0] % 2]
        diffs[0] += 1
        ps = T[bank][:, 0:n]
        mm(["IB"] + rd, bank, ps, T.IB[:], occ, True, False)
        mm(["NIB", rt], bank, ps, T.NIB[:], reps, False, True)
        act([bank], [otok], out, ps, ACT.Abs)

    def first(s):
        gather("s", ["L1U"], ["OCC1Ds"], T.OCC1[:, 0:192], T.L1U[:, 24 * s:24 * s + 12])
        gather("v", ["L1U"], ["OCC1Dv"], T.OCC1[:, 192:384], T.L1U[:, 24 * s + 12:24 * s + 24])
        cp(["P1A"], ["PLW1D"], T.PLW[:, 96:120], T.P1A[:, 24 * s:24 * s + 24])

    for s in range(S):
        arrivals = s > 0
        send = s + 1 < S
        H = 8 if arrivals else 6
        both = ("D", "R") if arrivals else ("D",)
        at, qt = "ARR%d" % s, "QR%d" % s
        arr = T[at] if arrivals else None
        PL1, PL2, PL3 = (["PLW%d%s" % (l, b) for b in both] for l in (1, 2, 3))
        if arrivals:
            outside("arr%d" % s, nland, [at])
            dma("y", [], ["XBqD"], T.XB[:, 0:96], T.qs[:, 96 * s:96 * s + 96])
            dma("y", [], ["OLDqD"], T.OLD[:, 384:480], T.qs[:, 96 * s:96 * s + 96])
        else:
            first(0)
            constants()

        wrapsum("WR", ["OCC1Ds", "OCC1Dv"], "SD", T.SD[:, 0:24], lambda r: T.OCC1[:, r:384:16], True, True)
        diff(["OCC1Ds", "OCC1Dv"], qt, T.OCC1[:, 0:384], T.QR[:, 6 * s:6 * s + 6, 0:64], 384, T.AB1[:, 0:384], "AB1D")
        places(["SD"], T.SD[:, 0:24], 24, T.PLW[:, 384:480], "PLW2D")
        cp(["PLW2D"], ["OF2D"], T.OF[:, 32:128], T.PLW[:, 384:480])
        gather("s", ["OF2D"], ["OCC2Ds"], T.OCC2[:, 0:768], T.OF[:, 32:80])
        gather("v", ["OF2D"], ["OCC2Dv"], T.OCC2[:, 768:1536], T.OF[:, 80:128])
        wrapsum("WR", ["OCC2Ds", "OCC2Dv"], "SD", T.SD[:, 32:128], lambda r: T.OCC2[:, r:1536:16], True, True)
        for c in range(3):
            diff((["OCC2Ds"], ["OCC2Ds", "OCC2Dv"], ["OCC2Dv"])[c], qt, T.OCC2[:, 512 * c:512 * c + 512],
                 T.QR[:, 6 * s + 2 * c:6 * s + 2 * c + 2, 0:256], 512, T.AB2[:, 512 * c:512 * c + 512], "AB2%d" % c)
        places(["SD"], T.SD[:, 32:128], 96, T.PLW[:, 1536:1920], "PLW3D")
        cp(["PLW3D"], ["OF3D"], T.OF[:, 160:544], T.PLW[:, 1536:1920])

        if arrivals:
            for k in range(2):
                sel(at, "QRR", T.QRR[:, k, 0:16], arr[:, 16 * k:16 * k + 16], [[0, 16]], A.is_equal, 0.0, 0, 0)
            w = 16
            while w < 512:
                sel("QRR", "QRR", T.QRR[:, :, w:2 * w], T.QRR[:, :, 0:w], [[0, 2], [0, w]], A.is_equal, 0.0, 0, 0)
                w *= 2
            dma("y", [at], ["XBqR"], T.XB[:, 96:128], arr[:])
            dma("y", [at], ["OLDqR"], T.OLD[:, 480:512], arr[:])
        if send:
            w, nt, lo = 16, "QR%d" % (s + 1), 6 * (s + 1)
            while w < 512:
                sel(nt, nt, T.QR[:, lo:lo + 6, w:2 * w], T.QR[:, lo:lo + 6, 0:w], [[0, 6], [0, w]], A.is_equal, 0.0, 0, 0)
                w *= 2
            dma("y", [nt], ["QX%d" % (s + 1)], T.QR[:, lo:lo + 6, 512:1024], T.QR[:, lo:lo + 6, 0:512])

        def df(hi):
            return T.DF[:, 1024 * hi:1024 * hi + 1024]

        def p_d(hi):
            if hi < 6:
                tt(["OF3D", qt, "QX%d" % s] + XR, ["DF%d" % hi], df(hi),
                   T.XB[:, 256:2304].indirect(T.OF[:, 160 + 64 * hi:224 + 64 * hi]), T.QR[:, 6 * s + hi, :], A.subtract)
            else:
                for c in range(2):
                    o, l = 1024 * hi + 512 * c, 160 + 64 * hi + 32 * c
                    tt(["OF3R", "QRR"] + XR, ["DF%d" % hi], T.DF[:, o:o + 512],
                       T.XB[:, 256:2304].indirect(T.OF[:, l:l + 32]), T.QRR[:, hi - 6, :], A.subtract)

        def p_s(hi):
            act(["DF%d" % hi], ["DF%d" % hi], df(hi), df(hi), ACT.Abs)

        def p_m(hi):
            wrapsum("EK", ["DF%d" % hi], "K3", T.K3[:, 64 * hi:64 * hi + 64], lambda r: T.DF[:, 1024 * hi + r:1024 * hi + 1024:16], False, False)

        def p_g(hi):
            k = 1024 * (hi % 2)
            gather("s", ["OF3D" if hi < 6 else "OF3R"], ["OCC3%d" % (hi % 2)], T.OCC3[:, k:k + 1024], T.OF[:, 160 + 64 * hi:224 + 64 * hi])

        def p_x(hi):
            if hi == 1:
                diff(["OCC1R"], "QRR", T.OCC1[:, 384:512], T.QRR[:, :, 0:64], 128, T.AB1[:, 384:512], "AB1R")
                return
            for c in range(2):
                o, k = 1024 * hi + 512 * c, 1024 * (hi % 2) + 512 * c
                reps = T.QR[:, 6 * s + hi, 0:512] if hi < 6 else T.QRR[:, hi - 6, :]
                diff(["OCC3%d" % (hi % 2)], qt if hi < 6 else "QRR", T.OCC3[:, k:k + 512], reps, 512, T.DF[:, o:o + 512], "DF%d" % hi)

        def p_rq():
            mm(["WBD", at], "SR", T.SR[:, 0:32], T.WBD[:], arr[:], True, True)
            tt(["MASK", "SR"], ["RS"], T.RS[:], T.SR[:, 0:32], T.MASK[:, 0:32], A.mult)
            tt(["MASK", at], ["RE"], T.RE[:], arr[:], T.MASK[:, 0:32], A.mult)
            for k in range(2):
                red(["RS"], ["RQ"], T.RQ[:, k:k + 1], T.RS[:, 16 * k:16 * k + 16], A.add)
            places(["RQ"], T.RQ[:], 2, T.PLW[:, 120:128], "PLW1R")
            cp(["PLW1R"], ["OF1R"], T.OF[:, 24:32], T.PLW[:, 120:128])
            gather("s", ["OF1R"], ["OCC1R"], T.OCC1[:, 384:512], T.OF[:, 24:32])
            wrapsum("WR", ["OCC1R"], "SR", T.SR[:, 32:40], lambda r: T.OCC1[:, 384 + r:512:16], True, True)
            for k in range(2):
                red(["RE"], ["RF"], T.RF[:, k:k + 1], T.RE[:, 16 * k:16 * k + 16], A.add)
            ts(["RF"], ["NEQ"], T.NEQ[:, 6:8], T.RF[:], 512.0, None, A.is_lt)

        def p_r2():
            places(["SR"], T.SR[:, 32:40], 8, T.PLW[:, 480:512], "PLW2R")
            cp(["PLW2R"], ["OF2R"], T.OF[:, 128:160], T.PLW[:, 480:512])
            gather("s", ["OF2R"], ["OCC2R"], T.OCC2[:, 1536:2048], T.OF[:, 128:160])
            wrapsum("WR", ["OCC2R"], "SR", T.SR[:, 64:96], lambda r: T.OCC2[:, 1536 + r:2048:16], True, True)
            diff(["OCC2R"], "QRR", T.OCC2[:, 1536:2048], T.QRR[:, :, 0:256], 512, T.AB2[:, 1536:2048], "AB23")

        def p_r3():
            places(["SR"], T.SR[:, 64:96], 32, T.PLW[:, 1920:2048], "PLW3R")
            cp(["PLW3R"], ["OF3R"], T.OF[:, 544:672], T.PLW[:, 1920:2048])

        def p_lc():
            ts(["IO16", "PMF"], ["MASK"], T.MASK[:], T.IO16[:], T.PMF[:, 0:1], None, A.is_equal)
            for t, c in enumerate((0.0, 128.0, 2304.0)):
                ts(["LN"], ["TRC"], T.TRC[:, 8 * t:8 * t + 8], T.LN[:], c, None, A.add)
                ts(["LN"], ["TRD"], T.TRD[:, 8 * t:8 * t + 8], T.LN[:], -1.0, 256.0 - c, A.mult, A.add)
            ts(["LN"], ["TL"], T.TL[:], T.LN[:], 128.0, None, A.add)
            ts(["TL"], ["NTL"], T.NTL[:], T.TL[:], -1.0, None, A.mult)
            vset("CL0", T.CL[:], 0.0)
            ts(["IO16", "PMF"], ["MKB"], T.MKB[:], T.IO16[:, 0:64], T.PMF[:, 0:1], -16.0, A.is_ge, A.mult)
            for i in range(S - 1):
                vset("SB%d" % i, T["SB%d" % i][:], 512.0)
            vset("OLDqR", T.OLD[:, 480:512], 0.0)
            sel("BDB", "LTB", T.LTB[:], T.BDB[:], [[1, 128]], A.is_gt, 0.0, 0, -1)

        def p_k3():
            mm(["IOFF", "ONE"], "K3", T.K3[:, 0:64 * H], T.IOFF[:], T.ONE[:, 0:64 * H], True, False)
            mm(["IH", "IX3"], "K3", T.K3[:, 0:64 * H], T.IH[:], T.IX3[:, 0:64 * H], False, False)

        def p_k1():
            mm(["IOFF", "ONE"], "K12", T.K12[:, 0:H, 0:4], T.IOFF[:], T.ONE[:, 0:4 * H], True, False)
            mm(["IH", "IX12"], "K12", T.K12[:, 0:H, 0:4], T.IH[:], T.IX12[:, 0:H, 0:4], False, False)
            wrapsum("EK", ["AB1" + b for b in both], "K12", T.K12[:, 0:H, 0:4], lambda r: T.AB1[:, r:64 * H:16], False, True)

        def p_fe():
            ts(["K12"], ["FE1"], T.FE1[:, 0:4 * H], T.K12[:, 0:H, 0:4], 0.0, None, A.is_ge)
            ts(["K12"], ["NH"], T.NH[:, 0:H, :], T.K12[:, 0:H, 0:4], OFFS + E11, None, A.is_ge)

        def p_fq():
            for a in range(4):
                tt(PL2 + PL1, ["FQ2"], T.FQ2[:, a:16 * H:4], T.PLW[:, 384 + a:384 + 16 * H:4], T.PLW[:, 96:96 + 4 * H], A.is_equal)

        def p_k2():
            mm(["IOFF", "ONE"], "K12", T.K12[:, 0:H, 4:20], T.IOFF[:], T.ONE[:, 0:16 * H], True, False)
            mm(["IH", "IX12"], "K12", T.K12[:, 0:H, 4:20], T.IH[:], T.IX12[:, 0:H, 4:20], False, False)
            wrapsum("EK", ["AB2%d" % i for i in range(H // 2)], "K12", T.K12[:, 0:H, 4:20], lambda r: T.AB2[:, r:256 * H:16], False, False)
            for a in range(4):
                mm(["IPEN", "FE1"], "K12", T.K12[:, 0:H, 4 + a:20:4], T.IPEN[:], T.FE1[:, 0:4 * H], False, False)
            mm(["IPEN", "FQ2"], "K12", T.K12[:, 0:H, 4:20], T.IPEN[:], T.FQ2[:, 0:16 * H], False, True)

        def p_fa():
            for f, c, o in (("FA", 0.0, A.is_ge), ("FB", OFFS, A.is_lt)):
                ts(["K12"], [f], T[f][:, 0:16 * H], T.K12[:, 0:H, 4:20], c, None, o)

        def p_p12():
            for a in range(4):
                for f in ("FA", "FB"):
                    mm(["IPEN", f], "K3", T.K3[:, a:64 * H:4], T.IPEN[:], T[f][:, 0:16 * H], False, False)

        def p_ph():
            cp(PL1, ["PH1"], T.PH[:, 0:4 * H], T.PLW[:, 96:96 + 4 * H])
            cp(PL2, ["PH2"], T.PH[:, 32:32 + 16 * H], T.PLW[:, 384:384 + 16 * H])
            mm(["IH", "PH2"], "OT", T.OT[:, 0:16 * H], T.IH[:], T.PH[:, 32:32 + 16 * H], True, True)
            for a in range(4):
                mm(["IH", "PH1"], "OT", T.OT[:, 128 + a:128 + 16 * H:4], T.IH[:], T.PH[:, 0:4 * H], True, True)

        def p_fp():
            for a in range(4):
                tt(PL3 + ["OT"], ["FP"], T.FP[:, a:64 * H:4], T.PLW[:, 1536 + a:1536 + 64 * H:4], T.OT[:, 0:16 * H], A.is_equal)

        def p_fg():
            for a in range(4):
                tt(PL3 + ["OT"], ["FG"], T.FG[:, a:64 * H:4], T.PLW[:, 1536 + a:1536 + 64 * H:4], T.OT[:, 128:128 + 16 * H], A.is_equal)

        def p_pp():
            mm(["IPEN", "FP"], "K3", T.K3[:, 0:64 * H], T.IPEN[:], T.FP[:, 0:64 * H], False, False)

        def p_pg():
            mm(["IPEN", "FG"], "K3", T.K3[:, 0:64 * H], T.IPEN[:], T.FG[:, 0:64 * H], False, True)

        def p_lv():
            tt(["NH"], ["N1"], T.N1[:], T.NH[:, :, 0:2], T.NH[:, :, 2:4], A.mult)
            tt(["N1"], ["LV"], T.LV[:], T.N1[:, :, 0], T.N1[:, :, 1], A.mult)
            tt(["LV", "NEQ"], ["LIVE"], T.LIVE[:], T.LV[:], T.NEQ[:], A.mult)
            ts(["LIVE"], ["MD"], T.MD[:], T.LIVE[:], -33554432.0, 16777216.0, A.mult, A.add)
            ts(["LIVE"], ["DEAD"], T.DEAD[:], T.LIVE[:], -16.0, 16.0, A.mult, A.add)

        def p_r12():
            for hi in range(H):
                red(["K12"], ["M12"], T.M12[:, hi:hi + 1], T.K12[:, hi, :], A.max)
            tt(["M12", "MD"], ["ML12"], T.ML12[:], T.M12[:], T.MD[:], A.max)

        by_block = {"d": p_d, "s": p_s, "m": p_m, "g": p_g, "x": p_x}
        whole = {"rq": p_rq, "r2": p_r2, "r3": p_r3, "lc": p_lc, "k3": p_k3, "k1": p_k1, "fe": p_fe, "fq": p_fq, "k2": p_k2, "fa": p_fa,
                 "p12": p_p12, "fp": p_fp, "fg": p_fg, "pp": p_pp, "ph": p_ph, "pg": p_pg, "lv": p_lv, "r12": p_r12}
        for w in ORDER.split():
            if w == "lc" and s > 0:
                continue
            if not arrivals and (w in ("rq", "r2", "r3", "x1") or w[0] in "dsmgx" and w[1:] in ("6", "7")):
                continue
            if w in whole:
                whole[w]()
            else:
                by_block[w[0]](int(w[1:]))

        for hi in range(H):
            red(["K3"], ["M3"], T.M3[:, hi:hi + 1], T.K3[:, 64 * hi:64 * hi + 64], A.max)
        tt(["ML12", "M3"], ["MI"], T.MI[:], T.ML12[:], T.M3[:], A.max)
        ts(["MI"], ["PG"], T.PG[:], T.MI[:], 4, 127, A.arith_shift_right, A.bitwise_and)
        ts(["MI"], ["PO"], T.PO[:, 0:8], T.MI[:], 2047, None, A.bitwise_and)
        ts(["MI"], ["PO"], T.PO[:, 8:16], T.MI[:], 2, 511, A.arith_shift_right, A.bitwise_and)
        tt(["PG", "BH"], ["PO"], T.PO[:, 16:24], T.PG[:], T.BH[:], A.max)
        cp(["PO"], ["POU"], T.POU[:], T.PO[:])
        ts(["MI"], ["NE"], T.NE[:], T.MI[:], 0.0, None, A.is_lt)
        tt(["POU", "MASK", "PLW0", "PLWA", "PLWB"] + PL1 + PL2 + PL3, ["SELM"],
           T.SELM[:], T.PLW[:, 0:2048].indirect(T.POU[:, 0:24]), T.MASK[:], A.mult)
        mm(["BDH", "SELM"], "OT", T.OT[:], T.BDH[:], T.SELM[:], True, True)
        for r in range(16):
            mm(["IH", "SELM"], "OW", T.OW[:, 0:24], T.IH[:], T.SELM[:, r:384:16], r == 0, r == 15)
        cp(["OT"], ["OTHH"], T.OTHH[:], T.OT[:])
        ts(["OW"], ["XL"], T.XL[:], T.OW[:, 0:24], 256.0, None, A.add)
        xall = XR + ["XBqD", "XBqR", "XBq", "XBt", "XBt2"]

        def own_blocks(h0):
            out = T.DB[:, 16 * h0:16 * h0 + 64]
            mm(["IB", "MKB"], "DB", out, T.IB[:], T.MKB[:], True, False)
            mm(["IB", "DEAD"], "DB", T.DB[:, 16 * h0:16 * h0 + 64:16], T.IB[:], T.DEAD[:, h0:h0 + 4], False, False)
            for k in range(9):
                mm(["IB"] + ["EQ%d" % h for h in range(h0, h0 + 4)], "DB", out, T.IB[:],
                   T.EQ[:, 8 * k + h0:8 * k + h0 + 4, 112:128], False, k == 8)

        for hi in range(7, -1, -1):
            n = 16 * (hi + 1)
            for t in range(3):
                ts(["OTHH", "OW"], ["EQ%d" % hi], T.EQ[:, 24 * t + hi:24 * t + hi + 17:8, 128 - n:128], T.OTHH[:, :, 0:n],
                   T.OW[:, 8 * t + hi:8 * t + hi + 1], None, A.is_equal)
            if hi >= SCAL:
                k = 9 * (hi - SCAL)
                op("s", ["EQ%d" % hi], ["CL%d" % hi, "JK%d" % hi], lambda e: e.activation(
                    T.JK[:, k:k + 9, 0:16 * hi], T.EQ[:, hi:72:8, 112 - 16 * hi:112], ACT.Copy, accum_out=T.CL[:, hi:hi + 1]))
            elif hi > 0:
                for k in range(9):
                    mm(["IB", "EQ%d" % hi], "DA", T.DA[:, 64 * hi:80 * hi], T.IB[:], T.EQ[:, 8 * k + hi, 112 - 16 * hi:112], k == 0, k == 8)
            if hi in (4, 0):
                own_blocks(hi)
        act(["XL"] + xall, ["OLD"], T.OLD[:, 0:384], T.XB[:, 0:2432].indirect(T.XL[:, 0:24]), ACT.Copy)
        tt(["OW", "TRD"], ["W1"], T.W1[:], T.OW[:, 0:24], T.TRD[:], A.add)
        for hi in range(SCAL - 1, 0, -1):
            red(["DA"], ["CL%d" % hi], T.CL[:, hi:hi + 1], T.DA[:, 64 * hi:80 * hi], A.max)
        for hi in range(7, -1, -1):
            red(["DB"], ["CFM"], T.CFM[:, hi:hi + 1], T.DB[:, 16 * hi:16 * hi + 16], A.max)
        tt(["CFM", "CL0"] + ["CL%d" % h for h in range(1, 8)], ["CFX"], T.CFX[:], T.CFM[:], T.CL[:], A.max)
        ts(["CFX"], ["GO"], T.GO[:], T.CFX[:], 0.5, None, A.is_lt)
        if send:
            tt(["GO", "NE"], ["ND"], T.ND[:], T.GO[:], T.NE[:], A.mult)
            mm(["IH", "NTL"], "OW", T.OW[:, 32:40], T.IH[:], T.NTL[:], True, False)
            mm(["LTB", "ND"], "OW", T.OW[:, 32:40], T.LTB[:], T.ND[:], False, False)
            for d in range(1, 8):
                mm(["BDB", "ND"], "OW", T.OW[:, 32 + d:40], T.BDB[:], T.ND[:, 0:8 - d], False, d == 7)
        for t in range(3):
            tt(["GO", "W1"], ["W2"], T.W2[:, 8 * t:8 * t + 8], T.W1[:, 8 * t:8 * t + 8], T.GO[:], A.mult)
        tt(["W2", "TRC"], ["W3"], T.W3[:], T.W2[:], T.TRC[:], A.add)
        cp(["W3"], ["DLU"], T.DLU[:], T.W3[:])
        op("v", ["DLU", "OLD", "OLDqD", "OLDqR"], xall,
           lambda e: e.tensor_copy(T.XB[:, 0:2432].indirect(T.DLU[:, 0:24]), T.OLD[:, 128:512]))
        if send:
            first(s + 1)
            sb = "SB%d" % s
            tt(["OW", "ND"], ["D2"], T.D2[:], T.OW[:, 32:40], T.ND[:], A.mult)
            tt(["D2", "TL"], ["D3"], T.D3[:], T.D2[:], T.TL[:], A.add)
            cp(["D3"], ["SLU"], T.SLU[:], T.D3[:])
            op("v", ["SLU", "OLD"], [sb], lambda e: e.tensor_copy(T[sb][:, 0:256].indirect(T.SLU[:, 0:8]), T.OLD[:, 0:128]))
            before("g", [sb], [])
            g.remote_dma(T["ARR%d" % (s + 1)][:], T[sb][:, 0:32], T.sem["arr%d" % (s + 1)], T.sem.sent, pid, rid, wire)
    dma("y", XR, ["y0"], T.y[:, 0:1024], T.XB[:, 256:1280])
    dma("s", XR, ["y1"], T.y[:, 1024:2048], T.XB[:, 1280:2304])
    g.wait_ge(T.sem.sent, nwire * (S - 1))
    finish()
